import numpy as np
import ml_dtypes


def mxq(x, axis, fmt="e4m3"):
    dtype, down = {"e4m3": (ml_dtypes.float8_e4m3fn, 7), "e5m2": (ml_dtypes.float8_e5m2, 14)}[fmt]
    v = np.moveaxis(np.asarray(x, np.float32).astype(ml_dtypes.bfloat16).astype(np.float64), axis, -1)
    blocks = v.reshape(v.shape[:-1] + (-1, 32))
    amax = np.abs(blocks).max(-1, keepdims=True)
    byte = np.maximum(np.where(amax > 0, np.frexp(amax)[1] - 1 + 127, 0) - down, 1)
    scale = np.exp2(byte - 127.0)
    codes = (blocks / scale).astype(np.float32).astype(dtype).astype(np.float64)
    return np.moveaxis((codes * scale).reshape(v.shape), -1, axis)


WIDE = False


def mx_kscale(k):
    if not WIDE:
        return np.ones(k)
    levels = np.array([10, -10, 5, -5, 0])
    if k % 512:
        return np.exp2(np.random.permutation(np.resize(levels, k // 32))).repeat(32)
    a = np.empty((k // 512, 16))
    for p in range(k // 512):
        a[p, :8] = np.random.permutation(np.resize(levels, 8))
        for g in range(8):
            far = levels[np.abs(levels - a[p, g]) >= 10]
            a[p, g + 8] = far[np.random.randint(len(far))]
    return np.exp2(a.ravel()).repeat(32)


def f64(x):
    return np.asarray(x).astype(np.float64)


def striped(idx):
    return np.tile(idx.reshape(-1, 16).T, (8, 1)).astype(np.uint16)


def unstriped(offs):
    return offs[:16].T.reshape(-1).astype(np.int64)


E2M1 = np.array([0.0, 0.5, 1.0, 1.5, 2.0, 3.0, 4.0, 6.0, -0.0, -0.5, -1.0, -1.5, -2.0, -3.0, -4.0, -6.0])


def pack_fp4(w):
    k, n = w.shape
    w = f64(np.asarray(w, np.float32).astype(ml_dtypes.bfloat16)).reshape(k // 32, 32, n)
    amax = np.abs(w).max(1)
    mant, ex = np.frexp(amax / 6.0)
    byte = np.clip(np.where(amax > 0, np.where(mant > 0.5, ex, ex - 1) + 127, 1), 1, 254)
    scaled = (w * np.exp2(127.0 - byte)[:, None, :]).reshape(k, n).astype(np.float32)
    c = np.ascontiguousarray(scaled.reshape(k // 512, 128, 4, n).transpose(0, 1, 3, 2)).astype(ml_dtypes.float4_e2m1fn).view(np.uint8) & 0xF
    words = (c[..., 0::2] | (c[..., 1::2] << 4)).reshape(k // 512, 128, 2 * n)
    return np.ascontiguousarray(words), np.ascontiguousarray(byte.astype(np.uint8).reshape(k // 512, 16, n))


def unpack_fp4(words, scales):
    g, _, n = scales.shape
    words = np.ascontiguousarray(words).reshape(g, 128, n, 2)
    nib = np.empty((g, 128, n, 4), np.uint8)
    nib[..., 0::2] = words & 0xF
    nib[..., 1::2] = words >> 4
    vals = E2M1[nib] * np.repeat(np.exp2(scales.astype(np.float64) - 127.0), 8, axis=1)[..., None]
    return vals.transpose(0, 1, 3, 2).reshape(g * 512, n)


def silu(v):
    return v / (1.0 + np.exp(-np.maximum(v, -700.0)))


K, T, S, H, N = 512, 2048, 1024, 512, 256
P = 2 ** 7


def setup_inputs():
    n = np.random.standard_normal
    s = mx_kscale(K)[:, None]
    u = mx_kscale(H)
    packed_xT = pack_fp4(n((K, T)) * s)
    return {
        "x_words": packed_xT[0],
        "x_scales": packed_xT[1],
        "gate": np.tile(np.random.uniform(0.2, 1.0, S), (P, 1)).astype(np.float32),
        "res": n((N, T)).astype(np.float32),
        "w1": (n((K, H)) / np.sqrt(K) / s).astype(np.float32),
        "w3": (n((K, H)) / np.sqrt(K) / s * u).astype(np.float32),
        "w2": (n((H, N)) / np.sqrt(H) / u[:, None]).astype(np.float32),
        "offs": striped(np.random.permutation(T)[:S]),
    }


def reference(x_words, x_scales, gate, res, w1, w3, w2, offs):
    r = f64(res)[:, unstriped(offs)]
    xq = unpack_fp4(x_words, x_scales)[:, unstriped(offs)]
    h = (silu(mxq(f64(w1), 0, "e4m3").T @ xq)) * ((mxq(f64(w3), 0, "e4m3").T @ xq))
    y = mxq(f64(w2), 0, "e4m3").T @ mxq(h, 0, "e4m3")
    out = f64(res).copy()
    out[:, unstriped(offs)] = r + y * f64(gate)[:1]
    return out

@@ -1,0 +1,199 @@
+from contextlib import ExitStack
+
+import concourse.mybir as mybir
+from concourse.masks import make_identity
+
+K, T, S, H, N = 512, 2048, 1024, 512, 256
+FLOPS = 2 * S * (2 * K * H + H * N)
+
+F32 = mybir.dt.float32
+BF16 = mybir.dt.bfloat16
+I32 = mybir.dt.int32
+U32 = mybir.dt.uint32
+U16 = mybir.dt.uint16
+U8 = mybir.dt.uint8
+FP8X4 = mybir.dt.float8_e4m3fn_x4
+FP4X4 = mybir.dt.float4_e2m1fn_x4
+ACT = mybir.ActivationFunctionType
+ALU = mybir.AluOpType
+
+P = 128
+PACK = 4
+TILES = S // P
+HALF = S // 2
+BLOCKS = N // P
+
+
+def tile_picked_modres_glusilu_p_kernel(
+    tc, x_words, x_scales, gate, res, w1, w3, w2, offs, out
+):
+    nc = tc.nc
+    with ExitStack() as ctx:
+        keep = ctx.enter_context(tc.tile_pool(name="keep", bufs=1))
+        psum = ctx.enter_context(tc.psum_pool(name="psum", bufs=2))
+
+        offsets = keep.tile([P, S // 16], U16, name="offsets")
+        nc.sync.dma_start(offsets[:], offs)
+
+        def offs_half(half):
+            return offsets[:, half * (HALF // 16) : (half + 1) * (HALF // 16)]
+
+        word_table = keep.tile([P, T], U16, name="word_table")
+        nc.sync.dma_start(word_table[:].bitcast(I32), x_words[0].bitcast(I32))
+
+        scale_table = keep.tile([P, T], U8, name="scale_table")
+        nc.gpsimd.memset(scale_table[:].bitcast(I32), 0)
+        for q in range(4):
+            nc.scalar.dma_start(
+                scale_table[32 * q : 32 * q + 4, :].bitcast(I32),
+                x_scales[0, 4 * q : 4 * q + 4, :].bitcast(I32),
+            )
+
+        raw = {}
+        for name, w in (("w1", w1), ("w3", w3)):
+            for half in range(2):
+                t_raw = keep.tile([P, PACK, H // 2], F32, name=f"{name}_raw{half}")
+                cols = slice(half * (H // 2), (half + 1) * (H // 2))
+                nc.sync.dma_start(t_raw[:], w.rearrange("(p j) c -> p j c", j=PACK)[:, :, cols])
+                raw[name, half] = t_raw
+
+        window = [keep.tile([P, T], F32, name=f"window{b}") for b in range(BLOCKS)]
+        nc.sync.dma_start(window[0][:], res[0:P, :])
+        w2_raw = keep.tile([P, PACK, N], F32, name="w2_raw")
+        nc.sync.dma_start(w2_raw[:], w2.rearrange("(p j) c -> p j c", j=PACK))
+        nc.sync.dma_start(window[1][:], res[P : 2 * P, :])
+
+        ident = keep.tile([P, P], F32, name="ident")
+        make_identity(nc, ident[:])
+        gate_rows = keep.tile([P, P], F32, name="gate_rows")
+        nc.gpsimd.memset(gate_rows[:], 0.0)
+        nc.sync.dma_start(gate_rows[0:TILES, :], gate[0].rearrange("(c p) -> c p", p=P))
+
+        warm = keep.tile([P, 1], F32, name="warm")
+        nc.scalar.activation(warm[:], ident[:, 0:1], ACT.Silu)
+
+        x_codes = keep.tile([P, S], U16, name="x_codes", align_bytes=64)
+        x_scale = keep.tile([P, S], U8, name="x_scale", align_bytes=64)
+        nc.vector.tensor_copy(x_scale[:], scale_table[:].indirect(offsets[:]))
+        for half in range(2):
+            nc.vector.tensor_copy(
+                x_codes[:, half * HALF : (half + 1) * HALF], word_table[:].indirect(offs_half(half))
+            )
+
+        codes = {}
+        scales = {}
+        for name in ("w1", "w3"):
+            grouped = keep.tile([P, PACK * H], BF16, name=f"{name}_grouped", align_bytes=64)
+            dst = grouped[:].rearrange("p (t m j) -> p m t j", t=PACK, j=PACK)
+            for half in range(2):
+                src = raw[name, half][:].rearrange("p j (m t) -> p m t j", t=PACK)
+                part = dst[:, half * (P // 2) : (half + 1) * (P // 2)]
+                if name == "w3" and half == 1:
+                    nc.vector.tensor_copy(part, src)
+                else:
+                    nc.scalar.copy(part, src)
+            codes[name] = keep.tile([P, H], U32, name=f"{name}_codes", align_bytes=64)
+            scales[name] = keep.tile([P, H], U8, name=f"{name}_scales", align_bytes=64)
+            nc.vector.quantize_mx(codes[name][:].bitcast(FP8X4), scales[name][:], grouped[:])
+
+        def first_product(name, c):
+            bank = psum.tile([P, PACK, P], F32, name=f"{name}_bank")
+            tok = slice(c * P, (c + 1) * P)
+            for t in range(PACK):
+                cols = slice(t * P, (t + 1) * P)
+                nc.tensor.matmul_mx(
+                    bank[:, t, :],
+                    lhsT=codes[name][:, cols].bitcast(FP8X4),
+                    lhsT_scale=scales[name][:, cols],
+                    rhs=x_codes[:, tok].bitcast(FP4X4),
+                    rhs_scale=x_scale[:, tok],
+                    start=True,
+                    stop=True,
+                )
+            return bank[:].rearrange("p t n -> p n t")
+
+        h_grouped = [keep.tile([P, HALF, PACK], BF16, name=f"h_grouped{i}", align_bytes=64) for i in range(2)]
+        h_codes = [keep.tile([P, HALF], U32, name=f"h_codes{i}", align_bytes=64) for i in range(2)]
+        h_scales = [keep.tile([P, HALF], U8, name=f"h_scales{i}", align_bytes=64) for i in range(2)]
+
+        def hidden(c):
+            half, within = divmod(c, TILES // 2)
+            act = keep.tile([P, P, PACK], F32, name=f"act{c}")
+            nc.scalar.activation(act[:], first_product("w1", c), ACT.Silu)
+            nc.vector.tensor_tensor(
+                h_grouped[half][:, within * P : (within + 1) * P, :], first_product("w3", c), act[:], ALU.mult
+            )
+
+        def quantize_hidden(half):
+            nc.vector.quantize_mx(
+                h_codes[half][:].bitcast(FP8X4),
+                h_scales[half][:],
+                h_grouped[half][:].rearrange("p n t -> p (n t)"),
+            )
+
+        for c in range(TILES // 2 + 1):
+            hidden(c)
+        quantize_hidden(0)
+
+        w2_grouped = keep.tile([P, N, PACK], BF16, name="w2_grouped", align_bytes=64)
+        nc.scalar.copy(w2_grouped[:], w2_raw[:].rearrange("p j c -> p c j"))
+        w2_codes = keep.tile([P, N], U32, name="w2_codes", align_bytes=64)
+        w2_scales = keep.tile([P, N], U8, name="w2_scales", align_bytes=64)
+        nc.vector.quantize_mx(
+            w2_codes[:].bitcast(FP8X4), w2_scales[:], w2_grouped[:].rearrange("p c j -> p (c j)")
+        )
+        gate_bank = psum.tile([P, HALF], F32, name="turn_bank")
+        nc.tensor.transpose(gate_bank[:, 0:P], gate_rows[:], ident[:])
+        gate_cols = keep.tile([P, TILES], F32, name="gate_cols")
+        nc.scalar.copy(gate_cols[:], gate_bank[:, 0:TILES])
+
+        for c in range(TILES // 2 + 1, TILES):
+            hidden(c)
+
+        picked = [keep.tile([P, S], F32, name=f"picked{b}") for b in range(BLOCKS)]
+        nc.vector.tensor_copy(picked[0][:], window[0][:].indirect(offsets[:]))
+        quantize_hidden(1)
+        nc.vector.tensor_copy(picked[1][:], window[1][:].indirect(offsets[:]))
+
+        gated = {}
+        for half in range(2):
+            by_token = keep.tile([P, TILES // 2, N], F32, name=f"by_token{half}")
+            for pair in range(TILES // 4):
+                bank = psum.tile([P, 2, N], F32, name="y_bank")
+                for e in range(2):
+                    within = 2 * pair + e
+                    tok = slice(within * P, (within + 1) * P)
+                    nc.tensor.matmul_mx(
+                        bank[:, e, :],
+                        lhsT=h_codes[half][:, tok].bitcast(FP8X4),
+                        lhsT_scale=h_scales[half][:, tok],
+                        rhs=w2_codes[:].bitcast(FP8X4),
+                        rhs_scale=w2_scales[:],
+                        start=True,
+                        stop=True,
+                    )
+                for e in range(2):
+                    within = 2 * pair + e
+                    c = half * (TILES // 2) + within
+                    nc.scalar.activation(
+                        by_token[:, within, :], bank[:, e, :], ACT.Copy, scale=gate_cols[:, c : c + 1]
+                    )
+            for b in range(BLOCKS):
+                bank = psum.tile([P, HALF], F32, name="turn_bank")
+                for within in range(TILES // 2):
+                    nc.tensor.transpose(
+                        bank[:, within * P : (within + 1) * P], by_token[:, within, b * P : (b + 1) * P], ident[:]
+                    )
+                gated[b, half] = keep.tile([P, HALF], F32, name=f"gated{b}{half}")
+                nc.scalar.copy(gated[b, half][:], bank[:])
+
+        for half in range(2):
+            for b in range(BLOCKS):
+                nc.vector.tensor_tensor(
+                    window[b][:].indirect(offs_half(half)),
+                    picked[b][:, half * HALF : (half + 1) * HALF],
+                    gated[b, half][:],
+                    ALU.add,
+                )
+                if half == 1:
+                    nc.sync.dma_start(out[b * P : (b + 1) * P, :], window[b][:])

@@ -22,6 +22,7 @@ PACK = 4
 TILES = S // P
 HALF = S // 2
 BLOCKS = N // P
+FIRST_BANKS = {"w1": 2, "w3": 4}
 
 
 def tile_picked_modres_glusilu_p_kernel(
@@ -44,18 +45,15 @@ def tile_picked_modres_glusilu_p_kernel(
         scale_table = keep.tile([P, T], U8, name="scale_table")
         nc.gpsimd.memset(scale_table[:].bitcast(I32), 0)
         for q in range(4):
-            nc.scalar.dma_start(
+            nc.sync.dma_start(
                 scale_table[32 * q : 32 * q + 4, :].bitcast(I32),
                 x_scales[0, 4 * q : 4 * q + 4, :].bitcast(I32),
             )
 
         raw = {}
         for name, w in (("w1", w1), ("w3", w3)):
-            for half in range(2):
-                t_raw = keep.tile([P, PACK, H // 2], F32, name=f"{name}_raw{half}")
-                cols = slice(half * (H // 2), (half + 1) * (H // 2))
-                nc.sync.dma_start(t_raw[:], w.rearrange("(p j) c -> p j c", j=PACK)[:, :, cols])
-                raw[name, half] = t_raw
+            raw[name] = keep.tile([P, PACK, H], F32, name=f"{name}_raw")
+            nc.sync.dma_start(raw[name][:], w.rearrange("(p j) c -> p j c", j=PACK))
 
         window = [keep.tile([P, T], F32, name=f"window{b}") for b in range(BLOCKS)]
         nc.sync.dma_start(window[0][:], res[0:P, :])
@@ -74,30 +72,31 @@ def tile_picked_modres_glusilu_p_kernel(
 
         x_codes = keep.tile([P, S], U16, name="x_codes", align_bytes=64)
         x_scale = keep.tile([P, S], U8, name="x_scale", align_bytes=64)
-        nc.vector.tensor_copy(x_scale[:], scale_table[:].indirect(offsets[:]))
         for half in range(2):
             nc.vector.tensor_copy(
                 x_codes[:, half * HALF : (half + 1) * HALF], word_table[:].indirect(offs_half(half))
             )
+        nc.vector.tensor_copy(x_scale[:], scale_table[:].indirect(offsets[:]))
 
         codes = {}
         scales = {}
         for name in ("w1", "w3"):
-            grouped = keep.tile([P, PACK * H], BF16, name=f"{name}_grouped", align_bytes=64)
+            grouped = keep.tile([P, PACK * H], BF16, name=f"{name}_grouped", tag=f"{name}_grouped", align_bytes=64)
             dst = grouped[:].rearrange("p (t m j) -> p m t j", t=PACK, j=PACK)
-            for half in range(2):
-                src = raw[name, half][:].rearrange("p j (m t) -> p m t j", t=PACK)
-                part = dst[:, half * (P // 2) : (half + 1) * (P // 2)]
-                if name == "w3" and half == 1:
-                    nc.vector.tensor_copy(part, src)
-                else:
-                    nc.scalar.copy(part, src)
+            src = raw[name][:].rearrange("p j (m t) -> p m t j", t=PACK)
+            if name == "w3":
+                nc.vector.tensor_copy(dst, src)
+            else:
+                nc.scalar.copy(dst, src)
             codes[name] = keep.tile([P, H], U32, name=f"{name}_codes", align_bytes=64)
             scales[name] = keep.tile([P, H], U8, name=f"{name}_scales", align_bytes=64)
             nc.vector.quantize_mx(codes[name][:].bitcast(FP8X4), scales[name][:], grouped[:])
 
+        picked = [keep.tile([P, S], F32, name="picked0", tag="w3_grouped", align_bytes=64)]
+        nc.vector.tensor_copy(picked[0][:], window[0][:].indirect(offsets[:]))
+
         def first_product(name, c):
-            bank = psum.tile([P, PACK, P], F32, name=f"{name}_bank")
+            bank = psum.tile([P, PACK, P], F32, name=f"{name}_bank", bufs=FIRST_BANKS[name])
             tok = slice(c * P, (c + 1) * P)
             for t in range(PACK):
                 cols = slice(t * P, (t + 1) * P)
@@ -118,7 +117,7 @@ def tile_picked_modres_glusilu_p_kernel(
 
         def hidden(c):
             half, within = divmod(c, TILES // 2)
-            act = keep.tile([P, P, PACK], F32, name=f"act{c}")
+            act = keep.tile([P, P, PACK], F32, name=f"act{c}", tag=f"act{c}")
             nc.scalar.activation(act[:], first_product("w1", c), ACT.Silu)
             nc.vector.tensor_tensor(
                 h_grouped[half][:, within * P : (within + 1) * P, :], first_product("w3", c), act[:], ALU.mult
@@ -142,7 +141,7 @@ def tile_picked_modres_glusilu_p_kernel(
         nc.vector.quantize_mx(
             w2_codes[:].bitcast(FP8X4), w2_scales[:], w2_grouped[:].rearrange("p c j -> p (c j)")
         )
-        gate_bank = psum.tile([P, HALF], F32, name="turn_bank")
+        gate_bank = psum.tile([P, HALF], F32, name="turn_bank", tag="late")
         nc.tensor.transpose(gate_bank[:, 0:P], gate_rows[:], ident[:])
         gate_cols = keep.tile([P, TILES], F32, name="gate_cols")
         nc.scalar.copy(gate_cols[:], gate_bank[:, 0:TILES])
@@ -150,16 +149,15 @@ def tile_picked_modres_glusilu_p_kernel(
         for c in range(TILES // 2 + 1, TILES):
             hidden(c)
 
-        picked = [keep.tile([P, S], F32, name=f"picked{b}") for b in range(BLOCKS)]
-        nc.vector.tensor_copy(picked[0][:], window[0][:].indirect(offsets[:]))
-        quantize_hidden(1)
+        picked.append(keep.tile([P, S], F32, name="picked1", tag=f"act{TILES - 1}"))
         nc.vector.tensor_copy(picked[1][:], window[1][:].indirect(offsets[:]))
+        quantize_hidden(1)
 
         gated = {}
         for half in range(2):
             by_token = keep.tile([P, TILES // 2, N], F32, name=f"by_token{half}")
             for pair in range(TILES // 4):
-                bank = psum.tile([P, 2, N], F32, name="y_bank")
+                bank = psum.tile([P, 2, N], F32, name="y_bank", tag="late")
                 for e in range(2):
                     within = 2 * pair + e
                     tok = slice(within * P, (within + 1) * P)
@@ -179,7 +177,7 @@ def tile_picked_modres_glusilu_p_kernel(
                         by_token[:, within, :], bank[:, e, :], ACT.Copy, scale=gate_cols[:, c : c + 1]
                     )
             for b in range(BLOCKS):
-                bank = psum.tile([P, HALF], F32, name="turn_bank")
+                bank = psum.tile([P, HALF], F32, name="turn_bank", tag="late")
                 for within in range(TILES // 2):
                     nc.tensor.transpose(
                         bank[:, within * P : (within + 1) * P], by_token[:, within, b * P : (b + 1) * P], ident[:]
@@ -196,4 +194,5 @@ def tile_picked_modres_glusilu_p_kernel(
                     ALU.add,
                 )
                 if half == 1:
-                    nc.sync.dma_start(out[b * P : (b + 1) * P, :], window[b][:])
+                    for queue, cols in ((nc.sync, slice(0, T // 2)), (nc.scalar, slice(T // 2, T))):
+                        queue.dma_start(out[b * P : (b + 1) * P, cols], window[b][:, cols])

@@ -22,6 +22,7 @@ PACK = 4
 TILES = S // P
 HALF = S // 2
 BLOCKS = N // P
+RUN = 2
 FIRST_BANKS = {"w1": 2, "w3": 4}
 
 
@@ -51,14 +52,16 @@ def tile_picked_modres_glusilu_p_kernel(
             )
 
         raw = {}
-        for name, w in (("w1", w1), ("w3", w3)):
+        for name, w in (("w3", w3), ("w1", w1)):
             raw[name] = keep.tile([P, PACK, H], F32, name=f"{name}_raw")
             nc.sync.dma_start(raw[name][:], w.rearrange("(p j) c -> p j c", j=PACK))
 
         window = [keep.tile([P, T], F32, name=f"window{b}") for b in range(BLOCKS)]
         nc.sync.dma_start(window[0][:], res[0:P, :])
         w2_raw = keep.tile([P, PACK, N], F32, name="w2_raw")
-        nc.sync.dma_start(w2_raw[:], w2.rearrange("(p j) c -> p j c", j=PACK))
+        w2_rows = w2.rearrange("(v t e) c -> e v t c", t=PACK, e=RUN)
+        for e in range(RUN):
+            nc.sync.dma_start(w2_raw[e:P:RUN, :, :], w2_rows[e])
         nc.sync.dma_start(window[1][:], res[P : 2 * P, :])
 
         ident = keep.tile([P, P], F32, name="ident")
@@ -82,9 +85,9 @@ def tile_picked_modres_glusilu_p_kernel(
         scales = {}
         for name in ("w1", "w3"):
             grouped = keep.tile([P, PACK * H], BF16, name=f"{name}_grouped", tag=f"{name}_grouped", align_bytes=64)
-            dst = grouped[:].rearrange("p (t m j) -> p m t j", t=PACK, j=PACK)
-            src = raw[name][:].rearrange("p j (m t) -> p m t j", t=PACK)
-            if name == "w3":
+            dst = grouped[:].rearrange("p (t v e j) -> p v t j e", t=PACK, e=RUN, j=PACK)
+            src = raw[name][:].rearrange("p j (v t e) -> p v t j e", t=PACK, e=RUN)
+            if name == "w1":
                 nc.vector.tensor_copy(dst, src)
             else:
                 nc.scalar.copy(dst, src)
@@ -92,7 +95,7 @@ def tile_picked_modres_glusilu_p_kernel(
             scales[name] = keep.tile([P, H], U8, name=f"{name}_scales", align_bytes=64)
             nc.vector.quantize_mx(codes[name][:].bitcast(FP8X4), scales[name][:], grouped[:])
 
-        picked = [keep.tile([P, S], F32, name="picked0", tag="w3_grouped", align_bytes=64)]
+        picked = [keep.tile([P, S], F32, name="picked0", tag="w1_grouped", align_bytes=64)]
         nc.vector.tensor_copy(picked[0][:], window[0][:].indirect(offsets[:]))
 
         def first_product(name, c):
@@ -135,7 +138,10 @@ def tile_picked_modres_glusilu_p_kernel(
         quantize_hidden(0)
 
         w2_grouped = keep.tile([P, N, PACK], BF16, name="w2_grouped", align_bytes=64)
-        nc.scalar.copy(w2_grouped[:], w2_raw[:].rearrange("p j c -> p c j"))
+        nc.scalar.copy(
+            w2_grouped[:].rearrange("p (c i) j -> p c j i", i=PACK),
+            w2_raw[:].rearrange("p j (c i) -> p c j i", i=PACK),
+        )
         w2_codes = keep.tile([P, N], U32, name="w2_codes", align_bytes=64)
         w2_scales = keep.tile([P, N], U8, name="w2_scales", align_bytes=64)
         nc.vector.quantize_mx(

@@ -114,50 +114,70 @@ def tile_picked_modres_glusilu_p_kernel(
                 )
             return bank[:].rearrange("p t n -> p n t")
 
-        h_grouped = [keep.tile([P, HALF, PACK], BF16, name=f"h_grouped{i}", align_bytes=64) for i in range(2)]
-        h_codes = [keep.tile([P, HALF], U32, name=f"h_codes{i}", align_bytes=64) for i in range(2)]
-        h_scales = [keep.tile([P, HALF], U8, name=f"h_scales{i}", align_bytes=64) for i in range(2)]
+        h_tags = ("h_first", "h_mid", "h_first")
+        h_tiles = ((0, 1, 2, 3), (4, 5), (6, 7))
+        h_grouped = {}
+        h_codes = keep.tile([P, S], U32, name="h_codes", align_bytes=64)
+        h_scales = keep.tile([P, S], U8, name="h_scales", align_bytes=64)
 
-        def hidden(c):
-            half, within = divmod(c, TILES // 2)
-            act = keep.tile([P, P, PACK], F32, name=f"act{c}", tag=f"act{c}")
+        def h_slot(c):
+            g = [c in tiles for tiles in h_tiles].index(True)
+            if g not in h_grouped:
+                h_grouped.setdefault(
+                    g,
+                    keep.tile([P, len(h_tiles[g]) * P, PACK], BF16, name=f"h_grouped{g}", tag=h_tags[g], align_bytes=64),
+                )
+            within = c - h_tiles[g][0]
+            return h_grouped[g][:, within * P : (within + 1) * P, :]
+
+        def hidden_on_vector(c):
+            act = keep.tile([P, P, PACK], F32, name=f"act{c}", tag=f"act{c}", align_bytes=64)
             nc.scalar.activation(act[:], first_product("w1", c), ACT.Silu)
-            nc.vector.tensor_tensor(
-                h_grouped[half][:, within * P : (within + 1) * P, :], first_product("w3", c), act[:], ALU.mult
-            )
+            nc.vector.tensor_tensor(h_slot(c), first_product("w3", c), act[:], ALU.mult)
 
-        def quantize_hidden(half):
+        def hidden_on_gpsimd(c):
+            act = keep.tile([P, P, PACK], F32, name=f"act{c}", tag=f"act{c}", align_bytes=64)
+            nc.scalar.activation(act[:], first_product("w1", c), ACT.Silu)
+            lin = keep.tile([P, P, PACK], F32, name=f"lin{c}")
+            nc.scalar.copy(lin[:], first_product("w3", c))
+            nc.gpsimd.tensor_tensor(h_slot(c), lin[:], act[:], ALU.mult)
+
+        def quantize_hidden(g):
+            tok = slice(h_tiles[g][0] * P, (h_tiles[g][-1] + 1) * P)
             nc.vector.quantize_mx(
-                h_codes[half][:].bitcast(FP8X4),
-                h_scales[half][:],
-                h_grouped[half][:].rearrange("p n t -> p (n t)"),
+                h_codes[:, tok].bitcast(FP8X4),
+                h_scales[:, tok],
+                h_grouped[g][:].rearrange("p n t -> p (n t)"),
             )
 
-        for c in range(TILES // 2 + 1):
-            hidden(c)
-        quantize_hidden(0)
-
-        w2_grouped = keep.tile([P, N, PACK], BF16, name="w2_grouped", align_bytes=64)
-        nc.scalar.copy(
-            w2_grouped[:].rearrange("p (c i) j -> p c j i", i=PACK),
-            w2_raw[:].rearrange("p j (c i) -> p c j i", i=PACK),
+        w2_grouped = keep.tile([P, N, PACK], BF16, name="w2_grouped", tag="w3_grouped", align_bytes=64)
+        nc.gpsimd.tensor_scalar(
+            w2_grouped[:], w2_raw[:].rearrange("p j c -> p c j"), 1.0, 0.0, ALU.mult, ALU.add
         )
-        w2_codes = keep.tile([P, N], U32, name="w2_codes", align_bytes=64)
+
+        hidden_on_gpsimd(4)
+        for c in range(4):
+            hidden_on_vector(c)
+
+        w2_codes = keep.tile([P, N], U32, name="w2_codes", tag="act2", align_bytes=64)
         w2_scales = keep.tile([P, N], U8, name="w2_scales", align_bytes=64)
         nc.vector.quantize_mx(
             w2_codes[:].bitcast(FP8X4), w2_scales[:], w2_grouped[:].rearrange("p c j -> p (c j)")
         )
+        quantize_hidden(0)
+
         gate_bank = psum.tile([P, HALF], F32, name="turn_bank", tag="late")
         nc.tensor.transpose(gate_bank[:, 0:P], gate_rows[:], ident[:])
         gate_cols = keep.tile([P, TILES], F32, name="gate_cols")
         nc.scalar.copy(gate_cols[:], gate_bank[:, 0:TILES])
 
-        for c in range(TILES // 2 + 1, TILES):
-            hidden(c)
-
-        picked.append(keep.tile([P, S], F32, name="picked1", tag=f"act{TILES - 1}"))
+        picked.append(keep.tile([P, S], F32, name="picked1", tag="act3", align_bytes=64))
         nc.vector.tensor_copy(picked[1][:], window[1][:].indirect(offsets[:]))
+        hidden_on_gpsimd(6)
+        hidden_on_gpsimd(7)
+        hidden_on_vector(5)
         quantize_hidden(1)
+        quantize_hidden(2)
 
         gated = {}
         for half in range(2):
@@ -166,11 +186,11 @@ def tile_picked_modres_glusilu_p_kernel(
                 bank = psum.tile([P, 2, N], F32, name="y_bank", tag="late")
                 for e in range(2):
                     within = 2 * pair + e
-                    tok = slice(within * P, (within + 1) * P)
+                    tok = slice(half * HALF + within * P, half * HALF + (within + 1) * P)
                     nc.tensor.matmul_mx(
                         bank[:, e, :],
-                        lhsT=h_codes[half][:, tok].bitcast(FP8X4),
-                        lhsT_scale=h_scales[half][:, tok],
+                        lhsT=h_codes[:, tok].bitcast(FP8X4),
+                        lhsT_scale=h_scales[:, tok],
                         rhs=w2_codes[:].bitcast(FP8X4),
                         rhs_scale=w2_scales[:],
                         start=True,

@@ -24,6 +24,7 @@ HALF = S // 2
 BLOCKS = N // P
 RUN = 2
 FIRST_BANKS = {"w1": 2, "w3": 4}
+GROUPED_ON = {"w1": "w1_grouped", "w3": "w1_raw"}
 
 
 def tile_picked_modres_glusilu_p_kernel(
@@ -52,8 +53,8 @@ def tile_picked_modres_glusilu_p_kernel(
             )
 
         raw = {}
-        for name, w in (("w3", w3), ("w1", w1)):
-            raw[name] = keep.tile([P, PACK, H], F32, name=f"{name}_raw")
+        for name, w in (("w1", w1), ("w3", w3)):
+            raw[name] = keep.tile([P, PACK, H], F32, name=f"{name}_raw", tag=f"{name}_raw", align_bytes=64)
             nc.sync.dma_start(raw[name][:], w.rearrange("(p j) c -> p j c", j=PACK))
 
         window = [keep.tile([P, T], F32, name=f"window{b}") for b in range(BLOCKS)]
@@ -84,22 +85,34 @@ def tile_picked_modres_glusilu_p_kernel(
         codes = {}
         scales = {}
         for name in ("w1", "w3"):
-            grouped = keep.tile([P, PACK * H], BF16, name=f"{name}_grouped", tag=f"{name}_grouped", align_bytes=64)
+            grouped = keep.tile([P, PACK * H], BF16, name=f"{name}_grouped", tag=GROUPED_ON[name], align_bytes=64)
             dst = grouped[:].rearrange("p (t v e j) -> p v t j e", t=PACK, e=RUN, j=PACK)
             src = raw[name][:].rearrange("p j (v t e) -> p v t j e", t=PACK, e=RUN)
+            nc.scalar.copy(dst[:, :, 0:2], src[:, :, 0:2])
             if name == "w1":
-                nc.vector.tensor_copy(dst, src)
+                for t in range(2, PACK):
+                    nc.gpsimd.tensor_scalar(
+                        grouped[:, t * H : (t + 1) * H].rearrange("p (v e j) -> p v e j", e=RUN, j=PACK),
+                        raw[name][:].rearrange("p j (v t e) -> p t v e j", t=PACK, e=RUN)[:, t],
+                        1.0,
+                        0.0,
+                        ALU.mult,
+                        ALU.add,
+                    )
             else:
-                nc.scalar.copy(dst, src)
+                nc.vector.tensor_copy(dst[:, :, 2:4], src[:, :, 2:4])
             codes[name] = keep.tile([P, H], U32, name=f"{name}_codes", align_bytes=64)
             scales[name] = keep.tile([P, H], U8, name=f"{name}_scales", align_bytes=64)
             nc.vector.quantize_mx(codes[name][:].bitcast(FP8X4), scales[name][:], grouped[:])
 
-        picked = [keep.tile([P, S], F32, name="picked0", tag="w1_grouped", align_bytes=64)]
+        picked = [keep.tile([P, S], F32, name="picked0", tag="w3_raw", align_bytes=64)]
         nc.vector.tensor_copy(picked[0][:], window[0][:].indirect(offsets[:]))
 
         def first_product(name, c):
-            bank = psum.tile([P, PACK, P], F32, name=f"{name}_bank", bufs=FIRST_BANKS[name])
+            if name == "w1" and c in (4, 0):
+                bank = psum.tile([P, PACK, P], F32, name="early_bank", tag="late")
+            else:
+                bank = psum.tile([P, PACK, P], F32, name=f"{name}_bank", bufs=FIRST_BANKS[name])
             tok = slice(c * P, (c + 1) * P)
             for t in range(PACK):
                 cols = slice(t * P, (t + 1) * P)
@@ -150,7 +163,7 @@ def tile_picked_modres_glusilu_p_kernel(
                 h_grouped[g][:].rearrange("p n t -> p (n t)"),
             )
 
-        w2_grouped = keep.tile([P, N, PACK], BF16, name="w2_grouped", tag="w3_grouped", align_bytes=64)
+        w2_grouped = keep.tile([P, N, PACK], BF16, name="w2_grouped", tag="w1_raw", align_bytes=64)
         nc.gpsimd.tensor_scalar(
             w2_grouped[:], w2_raw[:].rearrange("p j c -> p c j"), 1.0, 0.0, ALU.mult, ALU.add
         )
@@ -208,7 +221,8 @@ def tile_picked_modres_glusilu_p_kernel(
                     nc.tensor.transpose(
                         bank[:, within * P : (within + 1) * P], by_token[:, within, b * P : (b + 1) * P], ident[:]
                     )
-                gated[b, half] = keep.tile([P, HALF], F32, name=f"gated{b}{half}")
+                gated_tag = f"act{TILES - 1}" if b + half == 0 else f"gated{b}{half}"
+                gated[b, half] = keep.tile([P, HALF], F32, name=f"gated{b}{half}", tag=gated_tag, align_bytes=64)
                 nc.scalar.copy(gated[b, half][:], bank[:])
 
         for half in range(2):

@@ -59,7 +59,7 @@ def tile_picked_modres_glusilu_p_kernel(
 
         window = [keep.tile([P, T], F32, name=f"window{b}") for b in range(BLOCKS)]
         nc.sync.dma_start(window[0][:], res[0:P, :])
-        w2_raw = keep.tile([P, PACK, N], F32, name="w2_raw")
+        w2_raw = keep.tile([P, PACK, N], F32, name="w2_raw", tag="h_mid", align_bytes=64)
         w2_rows = w2.rearrange("(v t e) c -> e v t c", t=PACK, e=RUN)
         for e in range(RUN):
             nc.sync.dma_start(w2_raw[e:P:RUN, :, :], w2_rows[e])

@@ -221,7 +221,7 @@ def tile_picked_modres_glusilu_p_kernel(
                     nc.tensor.transpose(
                         bank[:, within * P : (within + 1) * P], by_token[:, within, b * P : (b + 1) * P], ident[:]
                     )
-                gated_tag = f"act{TILES - 1}" if b + half == 0 else f"gated{b}{half}"
+                gated_tag = f"act{TILES - BLOCKS + b}" if half == 0 else f"gated{b}{half}"
                 gated[b, half] = keep.tile([P, HALF], F32, name=f"gated{b}{half}", tag=gated_tag, align_bytes=64)
                 nc.scalar.copy(gated[b, half][:], bank[:])
 

@@ -1,7 +1,6 @@
 from contextlib import ExitStack
 
 import concourse.mybir as mybir
-from concourse.masks import make_identity
 
 K, T, S, H, N = 512, 2048, 1024, 512, 256
 FLOPS = 2 * S * (2 * K * H + H * N)
@@ -20,10 +19,10 @@ ALU = mybir.AluOpType
 P = 128
 PACK = 4
 TILES = S // P
-HALF = S // 2
+PIECE = 2 * P
+PIECES = S // PIECE
 BLOCKS = N // P
 RUN = 2
-FIRST_BANKS = {"w1": 2, "w3": 4}
 GROUPED_ON = {"w1": "w1_grouped", "w3": "w1_raw"}
 
 
@@ -33,13 +32,14 @@ def tile_picked_modres_glusilu_p_kernel(
     nc = tc.nc
     with ExitStack() as ctx:
         keep = ctx.enter_context(tc.tile_pool(name="keep", bufs=1))
+        staged = ctx.enter_context(tc.tile_pool(name="staged", bufs=1))
         psum = ctx.enter_context(tc.psum_pool(name="psum", bufs=2))
 
         offsets = keep.tile([P, S // 16], U16, name="offsets")
         nc.sync.dma_start(offsets[:], offs)
 
-        def offs_half(half):
-            return offsets[:, half * (HALF // 16) : (half + 1) * (HALF // 16)]
+        def entries(first, count):
+            return offsets[:, first // 16 : (first + count) // 16]
 
         word_table = keep.tile([P, T], U16, name="word_table")
         nc.sync.dma_start(word_table[:].bitcast(I32), x_words[0].bitcast(I32))
@@ -52,33 +52,37 @@ def tile_picked_modres_glusilu_p_kernel(
                 x_scales[0, 4 * q : 4 * q + 4, :].bitcast(I32),
             )
 
+        warm_in = keep.tile([P, 1], F32, name="warm_in")
+        nc.gpsimd.memset(warm_in[:], 0.0)
+        warm = keep.tile([P, 1], F32, name="warm")
+        nc.scalar.activation(warm[:], warm_in[:], ACT.Silu)
+
         raw = {}
         for name, w in (("w1", w1), ("w3", w3)):
-            raw[name] = keep.tile([P, PACK, H], F32, name=f"{name}_raw", tag=f"{name}_raw", align_bytes=64)
+            if name == "w1":
+                raw[name] = keep.tile([P, PACK, H], F32, name="w1_raw", tag="w1_raw", align_bytes=64)
+            else:
+                raw[name] = staged.tile([P, PACK, H], F32, name="w3_raw", offset=0)
             nc.sync.dma_start(raw[name][:], w.rearrange("(p j) c -> p j c", j=PACK))
 
-        window = [keep.tile([P, T], F32, name=f"window{b}") for b in range(BLOCKS)]
-        nc.sync.dma_start(window[0][:], res[0:P, :])
-        w2_raw = keep.tile([P, PACK, N], F32, name="w2_raw", tag="h_mid", align_bytes=64)
+        w2_raw = keep.tile([P, PACK, N], F32, name="w2_raw", align_bytes=64)
         w2_rows = w2.rearrange("(v t e) c -> e v t c", t=PACK, e=RUN)
         for e in range(RUN):
             nc.sync.dma_start(w2_raw[e:P:RUN, :, :], w2_rows[e])
+        window = [keep.tile([P, T], F32, name=f"window{b}") for b in range(BLOCKS)]
+        nc.sync.dma_start(window[0][:], res[0:P, :])
+        gate_rows = keep.tile([P, S], F32, name="gate_rows")
+        nc.sync.dma_start(gate_rows[:], gate)
+        table1 = keep.tile([P, T], F32, name="table1")
+        nc.sync.dma_start(table1[:], res[P : 2 * P, :])
         nc.sync.dma_start(window[1][:], res[P : 2 * P, :])
-
-        ident = keep.tile([P, P], F32, name="ident")
-        make_identity(nc, ident[:])
-        gate_rows = keep.tile([P, P], F32, name="gate_rows")
-        nc.gpsimd.memset(gate_rows[:], 0.0)
-        nc.sync.dma_start(gate_rows[0:TILES, :], gate[0].rearrange("(c p) -> c p", p=P))
-
-        warm = keep.tile([P, 1], F32, name="warm")
-        nc.scalar.activation(warm[:], ident[:, 0:1], ACT.Silu)
 
         x_codes = keep.tile([P, S], U16, name="x_codes", align_bytes=64)
         x_scale = keep.tile([P, S], U8, name="x_scale", align_bytes=64)
         for half in range(2):
             nc.vector.tensor_copy(
-                x_codes[:, half * HALF : (half + 1) * HALF], word_table[:].indirect(offs_half(half))
+                x_codes[:, half * (S // 2) : (half + 1) * (S // 2)],
+                word_table[:].indirect(entries(half * (S // 2), S // 2)),
             )
         nc.vector.tensor_copy(x_scale[:], scale_table[:].indirect(offsets[:]))
 
@@ -105,14 +109,8 @@ def tile_picked_modres_glusilu_p_kernel(
             scales[name] = keep.tile([P, H], U8, name=f"{name}_scales", align_bytes=64)
             nc.vector.quantize_mx(codes[name][:].bitcast(FP8X4), scales[name][:], grouped[:])
 
-        picked = [keep.tile([P, S], F32, name="picked0", tag="w3_raw", align_bytes=64)]
-        nc.vector.tensor_copy(picked[0][:], window[0][:].indirect(offsets[:]))
-
         def first_product(name, c):
-            if name == "w1" and c in (4, 0):
-                bank = psum.tile([P, PACK, P], F32, name="early_bank", tag="late")
-            else:
-                bank = psum.tile([P, PACK, P], F32, name=f"{name}_bank", bufs=FIRST_BANKS[name])
+            bank = psum.tile([P, PACK, P], F32, name=f"{name}_bank", bufs=3)
             tok = slice(c * P, (c + 1) * P)
             for t in range(PACK):
                 cols = slice(t * P, (t + 1) * P)
@@ -127,112 +125,123 @@ def tile_picked_modres_glusilu_p_kernel(
                 )
             return bank[:].rearrange("p t n -> p n t")
 
-        h_tags = ("h_first", "h_mid", "h_first")
-        h_tiles = ((0, 1, 2, 3), (4, 5), (6, 7))
-        h_grouped = {}
+        act_bytes = P * PACK * 4
+        h_at = TILES * act_bytes
+        h_bytes = PIECE * PACK * 2
+        h_grouped = [
+            staged.tile([P, PIECE, PACK], BF16, name=f"h_grouped{q}", offset=h_at + q * h_bytes, align_bytes=64)
+            for q in range(PIECES)
+        ]
         h_codes = keep.tile([P, S], U32, name="h_codes", align_bytes=64)
         h_scales = keep.tile([P, S], U8, name="h_scales", align_bytes=64)
+        picked = keep.tile([P, S], F32, name="picked")
+        summed = {}
 
-        def h_slot(c):
-            g = [c in tiles for tiles in h_tiles].index(True)
-            if g not in h_grouped:
-                h_grouped.setdefault(
-                    g,
-                    keep.tile([P, len(h_tiles[g]) * P, PACK], BF16, name=f"h_grouped{g}", tag=h_tags[g], align_bytes=64),
-                )
-            within = c - h_tiles[g][0]
-            return h_grouped[g][:, within * P : (within + 1) * P, :]
+        def piece(q, count=1):
+            return slice(q * PIECE, (q + count) * PIECE)
 
-        def hidden_on_vector(c):
-            act = keep.tile([P, P, PACK], F32, name=f"act{c}", tag=f"act{c}", align_bytes=64)
+        def hidden(c):
+            act = staged.tile([P, P, PACK], F32, name=f"act{c}", offset=c * act_bytes)
             nc.scalar.activation(act[:], first_product("w1", c), ACT.Silu)
-            nc.vector.tensor_tensor(h_slot(c), first_product("w3", c), act[:], ALU.mult)
+            slot = h_grouped[c // 2][:, (c % 2) * P : (c % 2 + 1) * P, :]
+            nc.vector.tensor_tensor(slot, first_product("w3", c), act[:], ALU.mult)
 
-        def hidden_on_gpsimd(c):
-            act = keep.tile([P, P, PACK], F32, name=f"act{c}", tag=f"act{c}", align_bytes=64)
-            nc.scalar.activation(act[:], first_product("w1", c), ACT.Silu)
-            lin = keep.tile([P, P, PACK], F32, name=f"lin{c}")
-            nc.scalar.copy(lin[:], first_product("w3", c))
-            nc.gpsimd.tensor_tensor(h_slot(c), lin[:], act[:], ALU.mult)
-
-        def quantize_hidden(g):
-            tok = slice(h_tiles[g][0] * P, (h_tiles[g][-1] + 1) * P)
+        def quantize_hidden(q):
             nc.vector.quantize_mx(
-                h_codes[:, tok].bitcast(FP8X4),
-                h_scales[:, tok],
-                h_grouped[g][:].rearrange("p n t -> p (n t)"),
+                h_codes[:, piece(q)].bitcast(FP8X4),
+                h_scales[:, piece(q)],
+                h_grouped[q][:].rearrange("p n t -> p (n t)"),
             )
+
+        def fetch_block0(q):
+            nc.scalar.activation(picked[:, piece(q)], window[0][:].indirect(entries(q * PIECE, PIECE)), ACT.Copy)
+
+        def second_product(dst, b, tok):
+            cols = slice(b * P, (b + 1) * P)
+            nc.tensor.matmul_mx(
+                dst,
+                lhsT=w2_codes[:, cols].bitcast(FP8X4),
+                lhsT_scale=w2_scales[:, cols],
+                rhs=h_codes[:, tok].bitcast(FP8X4),
+                rhs_scale=h_scales[:, tok],
+                start=True,
+                stop=True,
+            )
+
+        def gated_product(b, tok, gated, tag="y_bank", bufs=2):
+            bank = psum.tile([P, tok.stop - tok.start], F32, name="y_bank", tag=tag, bufs=bufs)
+            second_product(bank[:], b, tok)
+            nc.vector.tensor_tensor(gated[:], bank[:], gate_rows[:, tok], ALU.mult)
+            return gated
+
+        def sum_block1(q, gated):
+            summed[1, q] = keep.tile([P, PIECE], F32, name=f"summed1{q}")
+            nc.vector.tensor_tensor(summed[1, q][:], table1[:].indirect(entries(q * PIECE, PIECE)), gated, ALU.add)
+
+        def scatter_on_scalar(b, q):
+            nc.scalar.activation(window[b][:].indirect(entries(q * PIECE, PIECE)), summed[b, q][:], ACT.Copy)
+
+        def scatter_on_vector(q, gated):
+            nc.vector.tensor_tensor(
+                window[0][:].indirect(entries(q * PIECE, PIECE)), picked[:, piece(q)], gated, ALU.add
+            )
+
+        def store(b, queue):
+            for cols in (slice(0, T // 2), slice(T // 2, T)):
+                queue.dma_start(out[b * P : (b + 1) * P, cols], window[b][:, cols])
+
+        def gated1(q):
+            return gated_product(1, piece(q), keep.tile([P, PIECE], F32, name=f"gated1{q}"))
 
         w2_grouped = keep.tile([P, N, PACK], BF16, name="w2_grouped", tag="w1_raw", align_bytes=64)
         nc.gpsimd.tensor_scalar(
             w2_grouped[:], w2_raw[:].rearrange("p j c -> p c j"), 1.0, 0.0, ALU.mult, ALU.add
         )
-
-        hidden_on_gpsimd(4)
-        for c in range(4):
-            hidden_on_vector(c)
-
-        w2_codes = keep.tile([P, N], U32, name="w2_codes", tag="act2", align_bytes=64)
+        w2_codes = keep.tile([P, N], U32, name="w2_codes", align_bytes=64)
         w2_scales = keep.tile([P, N], U8, name="w2_scales", align_bytes=64)
+
+        hidden(0)
+        hidden(1)
         nc.vector.quantize_mx(
             w2_codes[:].bitcast(FP8X4), w2_scales[:], w2_grouped[:].rearrange("p c j -> p (c j)")
         )
         quantize_hidden(0)
+        hidden(2)
+        hidden(3)
 
-        gate_bank = psum.tile([P, HALF], F32, name="turn_bank", tag="late")
-        nc.tensor.transpose(gate_bank[:, 0:P], gate_rows[:], ident[:])
-        gate_cols = keep.tile([P, TILES], F32, name="gate_cols")
-        nc.scalar.copy(gate_cols[:], gate_bank[:, 0:TILES])
+        first_bank = psum.tile([P, BLOCKS, PIECE], F32, name="y_bank", tag="y_bank")
+        for b in range(BLOCKS):
+            second_product(first_bank[:, b, :], b, piece(0))
+        first_gated = keep.tile([P, BLOCKS, PIECE], F32, name="first_gated")
+        first_gate = gate_rows[:, piece(0)].unsqueeze(1).to_broadcast([P, BLOCKS, PIECE])
+        nc.vector.tensor_tensor(first_gated[:], first_bank[:], first_gate, ALU.mult)
 
-        picked.append(keep.tile([P, S], F32, name="picked1", tag="act3", align_bytes=64))
-        nc.vector.tensor_copy(picked[1][:], window[1][:].indirect(offsets[:]))
-        hidden_on_gpsimd(6)
-        hidden_on_gpsimd(7)
-        hidden_on_vector(5)
         quantize_hidden(1)
+        hidden(4)
+        for q in range(PIECES):
+            fetch_block0(q)
+        sum_block1(0, first_gated[:, 1, :])
+        hidden(5)
+        summed[0, 0] = staged.tile([P, PIECE], F32, name="summed00", offset=5 * act_bytes)
+        nc.vector.tensor_tensor(summed[0, 0][:], picked[:, piece(0)], first_gated[:, 0, :], ALU.add)
+        g1 = gated1(1)
         quantize_hidden(2)
-
-        gated = {}
-        for half in range(2):
-            by_token = keep.tile([P, TILES // 2, N], F32, name=f"by_token{half}")
-            for pair in range(TILES // 4):
-                bank = psum.tile([P, 2, N], F32, name="y_bank", tag="late")
-                for e in range(2):
-                    within = 2 * pair + e
-                    tok = slice(half * HALF + within * P, half * HALF + (within + 1) * P)
-                    nc.tensor.matmul_mx(
-                        bank[:, e, :],
-                        lhsT=h_codes[:, tok].bitcast(FP8X4),
-                        lhsT_scale=h_scales[:, tok],
-                        rhs=w2_codes[:].bitcast(FP8X4),
-                        rhs_scale=w2_scales[:],
-                        start=True,
-                        stop=True,
-                    )
-                for e in range(2):
-                    within = 2 * pair + e
-                    c = half * (TILES // 2) + within
-                    nc.scalar.activation(
-                        by_token[:, within, :], bank[:, e, :], ACT.Copy, scale=gate_cols[:, c : c + 1]
-                    )
-            for b in range(BLOCKS):
-                bank = psum.tile([P, HALF], F32, name="turn_bank", tag="late")
-                for within in range(TILES // 2):
-                    nc.tensor.transpose(
-                        bank[:, within * P : (within + 1) * P], by_token[:, within, b * P : (b + 1) * P], ident[:]
-                    )
-                gated_tag = f"act{TILES - BLOCKS + b}" if half == 0 else f"gated{b}{half}"
-                gated[b, half] = keep.tile([P, HALF], F32, name=f"gated{b}{half}", tag=gated_tag, align_bytes=64)
-                nc.scalar.copy(gated[b, half][:], bank[:])
-
-        for half in range(2):
-            for b in range(BLOCKS):
-                nc.vector.tensor_tensor(
-                    window[b][:].indirect(offs_half(half)),
-                    picked[b][:, half * HALF : (half + 1) * HALF],
-                    gated[b, half][:],
-                    ALU.add,
-                )
-                if half == 1:
-                    for queue, cols in ((nc.sync, slice(0, T // 2)), (nc.scalar, slice(T // 2, T))):
-                        queue.dma_start(out[b * P : (b + 1) * P, cols], window[b][:, cols])
+        hidden(6)
+        sum_block1(1, g1[:])
+        hidden(7)
+        g2 = gated1(2)
+        quantize_hidden(3)
+        sum_block1(2, g2[:])
+        g3 = gated1(3)
+        late_pair = staged.tile([P, 2 * PIECE], F32, name="late_pair", offset=h_at + 3 * h_bytes)
+        gated_product(0, piece(1, 2), late_pair, tag="w1_bank", bufs=3)
+        sum_block1(3, g3[:])
+        late_last = gated_product(0, piece(3), keep.tile([P, PIECE], F32, name="late_last"), tag="w1_bank", bufs=3)
+        scatter_on_scalar(0, 0)
+        for q in range(PIECES):
+            scatter_on_scalar(1, q)
+        store(1, nc.scalar)
+        scatter_on_vector(1, late_pair[:, 0:PIECE])
+        scatter_on_vector(2, late_pair[:, PIECE : 2 * PIECE])
+        scatter_on_vector(3, late_last[:])
+        store(0, nc.sync)

@@ -23,7 +23,7 @@ PIECE = 2 * P
 PIECES = S // PIECE
 BLOCKS = N // P
 RUN = 2
-GROUPED_ON = {"w1": "w1_grouped", "w3": "w1_raw"}
+EARLY = 3 * PIECE
 
 
 def tile_picked_modres_glusilu_p_kernel(
@@ -57,61 +57,82 @@ def tile_picked_modres_glusilu_p_kernel(
         warm = keep.tile([P, 1], F32, name="warm")
         nc.scalar.activation(warm[:], warm_in[:], ACT.Silu)
 
-        raw = {}
-        for name, w in (("w1", w1), ("w3", w3)):
-            if name == "w1":
-                raw[name] = keep.tile([P, PACK, H], F32, name="w1_raw", tag="w1_raw", align_bytes=64)
-            else:
-                raw[name] = staged.tile([P, PACK, H], F32, name="w3_raw", offset=0)
-            nc.sync.dma_start(raw[name][:], w.rearrange("(p j) c -> p j c", j=PACK))
+        w1_raw = keep.tile([P, PACK, H], F32, name="w1_raw")
+        nc.sync.dma_start(w1_raw[:], w1.rearrange("(p j) c -> p j c", j=PACK))
+        w3_raw = [
+            keep.tile([P, PACK, H // 2], F32, name="w3_raw0"),
+            staged.tile([P, PACK, H // 2 + 32], F32, name="w3_raw1", offset=7 * P * 2),
+        ]
+        for half in range(2):
+            cols = slice(half * (H // 2), (half + 1) * (H // 2))
+            nc.sync.dma_start(w3_raw[half][:, :, 0 : H // 2], w3.rearrange("(p j) c -> p j c", j=PACK)[:, :, cols])
 
         w2_raw = keep.tile([P, PACK, N], F32, name="w2_raw", align_bytes=64)
         w2_rows = w2.rearrange("(v t e) c -> e v t c", t=PACK, e=RUN)
         for e in range(RUN):
             nc.sync.dma_start(w2_raw[e:P:RUN, :, :], w2_rows[e])
         window = [keep.tile([P, T], F32, name=f"window{b}") for b in range(BLOCKS)]
-        nc.sync.dma_start(window[0][:], res[0:P, :])
         gate_rows = keep.tile([P, S], F32, name="gate_rows")
-        nc.sync.dma_start(gate_rows[:], gate)
+        nc.sync.dma_start(gate_rows[:, 0 : S // 2], gate[:, 0 : S // 2])
         table1 = keep.tile([P, T], F32, name="table1")
         nc.sync.dma_start(table1[:], res[P : 2 * P, :])
+        nc.sync.dma_start(window[0][:], res[0:P, :])
+        nc.sync.dma_start(gate_rows[:, S // 2 : S], gate[:, S // 2 : S])
         nc.sync.dma_start(window[1][:], res[P : 2 * P, :])
 
         x_codes = keep.tile([P, S], U16, name="x_codes", align_bytes=64)
-        x_scale = keep.tile([P, S], U8, name="x_scale", align_bytes=64)
+        x_scale = keep.tile([P, EARLY], U8, name="x_scale", align_bytes=64)
         for half in range(2):
             nc.vector.tensor_copy(
                 x_codes[:, half * (S // 2) : (half + 1) * (S // 2)],
                 word_table[:].indirect(entries(half * (S // 2), S // 2)),
             )
-        nc.vector.tensor_copy(x_scale[:], scale_table[:].indirect(offsets[:]))
+        nc.vector.tensor_copy(x_scale[:], scale_table[:].indirect(entries(0, EARLY)))
 
+        def cast(copy, grouped, source, first_run, places):
+            runs = source.shape[2] // (PACK * RUN)
+            dst = grouped[:].rearrange("p (t v e j) -> p v t j e", t=PACK, e=RUN, j=PACK)
+            src = source.rearrange("p j (v t e) -> p v t j e", t=PACK, e=RUN)
+            copy(dst[:, first_run : first_run + runs, places], src[:, :, places])
+
+        grouped = {
+            "w1": keep.tile([P, PACK * H], BF16, name="w1_grouped", tag="w1_grouped", align_bytes=64),
+            "w3": keep.tile([P, PACK * H], BF16, name="w3_grouped", tag="w3_grouped", align_bytes=64),
+        }
         codes = {}
         scales = {}
-        for name in ("w1", "w3"):
-            grouped = keep.tile([P, PACK * H], BF16, name=f"{name}_grouped", tag=GROUPED_ON[name], align_bytes=64)
-            dst = grouped[:].rearrange("p (t v e j) -> p v t j e", t=PACK, e=RUN, j=PACK)
-            src = raw[name][:].rearrange("p j (v t e) -> p v t j e", t=PACK, e=RUN)
-            nc.scalar.copy(dst[:, :, 0:2], src[:, :, 0:2])
-            if name == "w1":
-                for t in range(2, PACK):
-                    nc.gpsimd.tensor_scalar(
-                        grouped[:, t * H : (t + 1) * H].rearrange("p (v e j) -> p v e j", e=RUN, j=PACK),
-                        raw[name][:].rearrange("p j (v t e) -> p t v e j", t=PACK, e=RUN)[:, t],
-                        1.0,
-                        0.0,
-                        ALU.mult,
-                        ALU.add,
-                    )
-            else:
-                nc.vector.tensor_copy(dst[:, :, 2:4], src[:, :, 2:4])
+
+        def quantize_first(name):
             codes[name] = keep.tile([P, H], U32, name=f"{name}_codes", align_bytes=64)
             scales[name] = keep.tile([P, H], U8, name=f"{name}_scales", align_bytes=64)
-            nc.vector.quantize_mx(codes[name][:].bitcast(FP8X4), scales[name][:], grouped[:])
+            nc.vector.quantize_mx(codes[name][:].bitcast(FP8X4), scales[name][:], grouped[name][:])
+
+        half_runs = H // (2 * PACK * RUN)
+        cast(nc.scalar.copy, grouped["w1"], w1_raw[:], 0, slice(0, 2))
+        for t in range(2, PACK):
+            nc.gpsimd.tensor_scalar(
+                grouped["w1"][:, t * H : (t + 1) * H].rearrange("p (v e j) -> p v e j", e=RUN, j=PACK),
+                w1_raw[:].rearrange("p j (v t e) -> p t v e j", t=PACK, e=RUN)[:, t],
+                1.0,
+                0.0,
+                ALU.mult,
+                ALU.add,
+            )
+        quantize_first("w1")
+        x_scale_late = keep.tile([P, S - EARLY], U8, name="x_scale_late", tag="w1_grouped", align_bytes=64)
+        nc.vector.tensor_copy(x_scale_late[:], scale_table[:].indirect(entries(EARLY, S - EARLY)))
+        cast(nc.scalar.copy, grouped["w3"], w3_raw[0][:], 0, slice(0, 4))
+        cast(nc.scalar.copy, grouped["w3"], w3_raw[1][:, :, 0 : H // 2], half_runs, slice(0, 2))
+        cast(nc.vector.tensor_copy, grouped["w3"], w3_raw[1][:, :, 0 : H // 2], half_runs, slice(2, 4))
+        quantize_first("w3")
 
         def first_product(name, c):
-            bank = psum.tile([P, PACK, P], F32, name=f"{name}_bank", bufs=3)
+            bank = psum.tile([P, PACK, P], F32, name=f"{name}_bank", bufs=4)
             tok = slice(c * P, (c + 1) * P)
+            if tok.start < EARLY:
+                tok_scale = x_scale[:, tok]
+            else:
+                tok_scale = x_scale_late[:, tok.start - EARLY : tok.stop - EARLY]
             for t in range(PACK):
                 cols = slice(t * P, (t + 1) * P)
                 nc.tensor.matmul_mx(
@@ -119,7 +140,7 @@ def tile_picked_modres_glusilu_p_kernel(
                     lhsT=codes[name][:, cols].bitcast(FP8X4),
                     lhsT_scale=scales[name][:, cols],
                     rhs=x_codes[:, tok].bitcast(FP4X4),
-                    rhs_scale=x_scale[:, tok],
+                    rhs_scale=tok_scale,
                     start=True,
                     stop=True,
                 )
@@ -128,23 +149,28 @@ def tile_picked_modres_glusilu_p_kernel(
         act_bytes = P * PACK * 4
         h_at = TILES * act_bytes
         h_bytes = PIECE * PACK * 2
-        h_grouped = [
-            staged.tile([P, PIECE, PACK], BF16, name=f"h_grouped{q}", offset=h_at + q * h_bytes, align_bytes=64)
-            for q in range(PIECES)
-        ]
+        h_grouped = {}
         h_codes = keep.tile([P, S], U32, name="h_codes", align_bytes=64)
         h_scales = keep.tile([P, S], U8, name="h_scales", align_bytes=64)
-        picked = keep.tile([P, S], F32, name="picked")
+        picked = staged.tile([P, S], F32, name="picked", offset=act_bytes // 2)
         summed = {}
 
         def piece(q, count=1):
             return slice(q * PIECE, (q + count) * PIECE)
 
+        act = {}
+
+        def silu(c):
+            act[c] = staged.tile([P, P, PACK], F32, name=f"act{c}", offset=c * act_bytes)
+            nc.scalar.activation(act[c][:], first_product("w1", c), ACT.Silu)
+
         def hidden(c):
-            act = staged.tile([P, P, PACK], F32, name=f"act{c}", offset=c * act_bytes)
-            nc.scalar.activation(act[:], first_product("w1", c), ACT.Silu)
+            if c % 2 == 0:
+                h_grouped[c // 2] = staged.tile(
+                    [P, PIECE, PACK], BF16, name=f"h_grouped{c // 2}", offset=h_at + c // 2 * h_bytes, align_bytes=64
+                )
             slot = h_grouped[c // 2][:, (c % 2) * P : (c % 2 + 1) * P, :]
-            nc.vector.tensor_tensor(slot, first_product("w3", c), act[:], ALU.mult)
+            nc.vector.tensor_tensor(slot, first_product("w3", c), act[c][:], ALU.mult)
 
         def quantize_hidden(q):
             nc.vector.quantize_mx(
@@ -153,95 +179,90 @@ def tile_picked_modres_glusilu_p_kernel(
                 h_grouped[q][:].rearrange("p n t -> p (n t)"),
             )
 
-        def fetch_block0(q):
-            nc.scalar.activation(picked[:, piece(q)], window[0][:].indirect(entries(q * PIECE, PIECE)), ACT.Copy)
-
-        def second_product(dst, b, tok):
-            cols = slice(b * P, (b + 1) * P)
-            nc.tensor.matmul_mx(
-                dst,
-                lhsT=w2_codes[:, cols].bitcast(FP8X4),
-                lhsT_scale=w2_scales[:, cols],
-                rhs=h_codes[:, tok].bitcast(FP8X4),
-                rhs_scale=h_scales[:, tok],
-                start=True,
-                stop=True,
-            )
-
-        def gated_product(b, tok, gated, tag="y_bank", bufs=2):
-            bank = psum.tile([P, tok.stop - tok.start], F32, name="y_bank", tag=tag, bufs=bufs)
-            second_product(bank[:], b, tok)
-            nc.vector.tensor_tensor(gated[:], bank[:], gate_rows[:, tok], ALU.mult)
+        def second_product(blocks, tok, gated):
+            width = tok.stop - tok.start
+            bank = psum.tile([P, len(blocks), width], F32, name="y_bank", tag="w1_bank", bufs=4)
+            for place, b in enumerate(blocks):
+                cols = slice(b * P, (b + 1) * P)
+                nc.tensor.matmul_mx(
+                    bank[:, place, :],
+                    lhsT=w2_codes[:, cols].bitcast(FP8X4),
+                    lhsT_scale=w2_scales[:, cols],
+                    rhs=h_codes[:, tok].bitcast(FP8X4),
+                    rhs_scale=h_scales[:, tok],
+                    start=True,
+                    stop=True,
+                )
+            weights = gate_rows[:, tok].unsqueeze(1).to_broadcast([P, len(blocks), width])
+            nc.vector.tensor_tensor(gated[:], bank[:], weights, ALU.mult)
             return gated
 
+        def gated_block1(q):
+            return second_product((1,), piece(q), keep.tile([P, 1, PIECE], F32, name=f"gated1{q}"))
+
+        def listed(tok):
+            return entries(tok.start, tok.stop - tok.start)
+
+        def fetch_block0(tok):
+            nc.scalar.activation(picked[:, tok], window[0][:].indirect(listed(tok)), ACT.Copy)
+
         def sum_block1(q, gated):
-            summed[1, q] = keep.tile([P, PIECE], F32, name=f"summed1{q}")
-            nc.vector.tensor_tensor(summed[1, q][:], table1[:].indirect(entries(q * PIECE, PIECE)), gated, ALU.add)
+            summed[q] = keep.tile([P, PIECE], F32, name=f"summed{q}")
+            nc.vector.tensor_tensor(summed[q][:], table1[:].indirect(listed(piece(q))), gated, ALU.add)
 
-        def scatter_on_scalar(b, q):
-            nc.scalar.activation(window[b][:].indirect(entries(q * PIECE, PIECE)), summed[b, q][:], ACT.Copy)
-
-        def scatter_on_vector(q, gated):
-            nc.vector.tensor_tensor(
-                window[0][:].indirect(entries(q * PIECE, PIECE)), picked[:, piece(q)], gated, ALU.add
-            )
+        def scatter_on_vector(tok, gated):
+            nc.vector.tensor_tensor(window[0][:].indirect(listed(tok)), picked[:, tok], gated, ALU.add)
 
         def store(b, queue):
             for cols in (slice(0, T // 2), slice(T // 2, T)):
                 queue.dma_start(out[b * P : (b + 1) * P, cols], window[b][:, cols])
 
-        def gated1(q):
-            return gated_product(1, piece(q), keep.tile([P, PIECE], F32, name=f"gated1{q}"))
-
-        w2_grouped = keep.tile([P, N, PACK], BF16, name="w2_grouped", tag="w1_raw", align_bytes=64)
+        w2_grouped = keep.tile([P, N, PACK], BF16, name="w2_grouped", tag="w3_grouped", align_bytes=64)
         nc.gpsimd.tensor_scalar(
             w2_grouped[:], w2_raw[:].rearrange("p j c -> p c j"), 1.0, 0.0, ALU.mult, ALU.add
         )
         w2_codes = keep.tile([P, N], U32, name="w2_codes", align_bytes=64)
         w2_scales = keep.tile([P, N], U8, name="w2_scales", align_bytes=64)
 
+        for c in range(4):
+            silu(c)
         hidden(0)
         hidden(1)
+        for c in range(4, TILES):
+            silu(c)
         nc.vector.quantize_mx(
             w2_codes[:].bitcast(FP8X4), w2_scales[:], w2_grouped[:].rearrange("p c j -> p (c j)")
         )
         quantize_hidden(0)
         hidden(2)
+        fetch_block0(piece(0))
+        fetch_block0(piece(1, PIECES - 1))
         hidden(3)
-
-        first_bank = psum.tile([P, BLOCKS, PIECE], F32, name="y_bank", tag="y_bank")
-        for b in range(BLOCKS):
-            second_product(first_bank[:, b, :], b, piece(0))
-        first_gated = keep.tile([P, BLOCKS, PIECE], F32, name="first_gated")
-        first_gate = gate_rows[:, piece(0)].unsqueeze(1).to_broadcast([P, BLOCKS, PIECE])
-        nc.vector.tensor_tensor(first_gated[:], first_bank[:], first_gate, ALU.mult)
-
+        first = keep.tile([P, BLOCKS, PIECE], F32, name="first")
+        second_product((0, 1), piece(0), first)
+        shared_sum = keep.tile([P, PIECE], F32, name="shared_sum")
+        nc.gpsimd.tensor_tensor(shared_sum[:], picked[:, piece(0)], first[:, 0, :], ALU.add)
         quantize_hidden(1)
+        sum_block1(0, first[:, 1, :])
         hidden(4)
-        for q in range(PIECES):
-            fetch_block0(q)
-        sum_block1(0, first_gated[:, 1, :])
+        g1 = gated_block1(1)
         hidden(5)
-        summed[0, 0] = staged.tile([P, PIECE], F32, name="summed00", offset=5 * act_bytes)
-        nc.vector.tensor_tensor(summed[0, 0][:], picked[:, piece(0)], first_gated[:, 0, :], ALU.add)
-        g1 = gated1(1)
+        sum_block1(1, g1[:, 0, :])
         quantize_hidden(2)
         hidden(6)
-        sum_block1(1, g1[:])
         hidden(7)
-        g2 = gated1(2)
+        g2 = gated_block1(2)
         quantize_hidden(3)
-        sum_block1(2, g2[:])
-        g3 = gated1(3)
-        late_pair = staged.tile([P, 2 * PIECE], F32, name="late_pair", offset=h_at + 3 * h_bytes)
-        gated_product(0, piece(1, 2), late_pair, tag="w1_bank", bufs=3)
-        sum_block1(3, g3[:])
-        late_last = gated_product(0, piece(3), keep.tile([P, PIECE], F32, name="late_last"), tag="w1_bank", bufs=3)
-        scatter_on_scalar(0, 0)
+        sum_block1(2, g2[:, 0, :])
+        late_pair = staged.tile([P, 1, 2 * PIECE], F32, name="late_pair", offset=h_at + 3 * h_bytes)
+        second_product((0,), piece(1, 2), late_pair)
+        g3 = gated_block1(3)
+        late_last = second_product((0,), piece(3), keep.tile([P, 1, PIECE], F32, name="late_last"))
+        sum_block1(3, g3[:, 0, :])
+        nc.scalar.activation(window[0][:].indirect(listed(piece(0))), shared_sum[:], ACT.Copy)
         for q in range(PIECES):
-            scatter_on_scalar(1, q)
+            nc.scalar.activation(window[1][:].indirect(listed(piece(q))), summed[q][:], ACT.Copy)
         store(1, nc.scalar)
-        scatter_on_vector(1, late_pair[:, 0:PIECE])
-        scatter_on_vector(2, late_pair[:, PIECE : 2 * PIECE])
-        scatter_on_vector(3, late_last[:])
+        scatter_on_vector(piece(3), late_last[:, 0, :])
+        scatter_on_vector(piece(1, 2), late_pair[:, 0, :])
         store(0, nc.sync)

@@ -23,6 +23,7 @@ PIECE = 2 * P
 PIECES = S // PIECE
 BLOCKS = N // P
 RUN = 2
+LONG = 384
 EARLY = 3 * PIECE
 
 
@@ -73,12 +74,9 @@ def tile_picked_modres_glusilu_p_kernel(
             nc.sync.dma_start(w2_raw[e:P:RUN, :, :], w2_rows[e])
         window = [keep.tile([P, T], F32, name=f"window{b}") for b in range(BLOCKS)]
         gate_rows = keep.tile([P, S], F32, name="gate_rows")
-        nc.sync.dma_start(gate_rows[:, 0 : S // 2], gate[:, 0 : S // 2])
-        table1 = keep.tile([P, T], F32, name="table1")
-        nc.sync.dma_start(table1[:], res[P : 2 * P, :])
-        nc.sync.dma_start(window[0][:], res[0:P, :])
-        nc.sync.dma_start(gate_rows[:, S // 2 : S], gate[:, S // 2 : S])
-        nc.sync.dma_start(window[1][:], res[P : 2 * P, :])
+        nc.sync.dma_start(gate_rows[:], gate)
+        for b in range(BLOCKS):
+            nc.sync.dma_start(window[b][:], res[b * P : (b + 1) * P, :])
 
         x_codes = keep.tile([P, S], U16, name="x_codes", align_bytes=64)
         x_scale = keep.tile([P, EARLY], U8, name="x_scale", align_bytes=64)
@@ -149,11 +147,13 @@ def tile_picked_modres_glusilu_p_kernel(
         act_bytes = P * PACK * 4
         h_at = TILES * act_bytes
         h_bytes = PIECE * PACK * 2
+        gap = PIECE * 4
+        h_offset = [h_at, h_at + h_bytes, h_at + 2 * h_bytes, h_at + 3 * h_bytes + gap]
         h_grouped = {}
         h_codes = keep.tile([P, S], U32, name="h_codes", align_bytes=64)
         h_scales = keep.tile([P, S], U8, name="h_scales", align_bytes=64)
         picked = staged.tile([P, S], F32, name="picked", offset=act_bytes // 2)
-        summed = {}
+        summed = keep.tile([P, S], F32, name="summed")
 
         def piece(q, count=1):
             return slice(q * PIECE, (q + count) * PIECE)
@@ -167,7 +167,7 @@ def tile_picked_modres_glusilu_p_kernel(
         def hidden(c):
             if c % 2 == 0:
                 h_grouped[c // 2] = staged.tile(
-                    [P, PIECE, PACK], BF16, name=f"h_grouped{c // 2}", offset=h_at + c // 2 * h_bytes, align_bytes=64
+                    [P, PIECE, PACK], BF16, name=f"h_grouped{c // 2}", offset=h_offset[c // 2], align_bytes=64
                 )
             slot = h_grouped[c // 2][:, (c % 2) * P : (c % 2 + 1) * P, :]
             nc.vector.tensor_tensor(slot, first_product("w3", c), act[c][:], ALU.mult)
@@ -179,39 +179,30 @@ def tile_picked_modres_glusilu_p_kernel(
                 h_grouped[q][:].rearrange("p n t -> p (n t)"),
             )
 
-        def second_product(blocks, tok, gated):
-            width = tok.stop - tok.start
-            bank = psum.tile([P, len(blocks), width], F32, name="y_bank", tag="w1_bank", bufs=4)
-            for place, b in enumerate(blocks):
-                cols = slice(b * P, (b + 1) * P)
-                nc.tensor.matmul_mx(
-                    bank[:, place, :],
-                    lhsT=w2_codes[:, cols].bitcast(FP8X4),
-                    lhsT_scale=w2_scales[:, cols],
-                    rhs=h_codes[:, tok].bitcast(FP8X4),
-                    rhs_scale=h_scales[:, tok],
-                    start=True,
-                    stop=True,
-                )
-            weights = gate_rows[:, tok].unsqueeze(1).to_broadcast([P, len(blocks), width])
-            nc.vector.tensor_tensor(gated[:], bank[:], weights, ALU.mult)
-            return gated
-
-        def gated_block1(q):
-            return second_product((1,), piece(q), keep.tile([P, 1, PIECE], F32, name=f"gated1{q}"))
+        def second_product(b, tok, gated):
+            bank = psum.tile([P, tok.stop - tok.start], F32, name="y_bank", tag="w1_bank", bufs=4)
+            cols = slice(b * P, (b + 1) * P)
+            nc.tensor.matmul_mx(
+                bank[:],
+                lhsT=w2_codes[:, cols].bitcast(FP8X4),
+                lhsT_scale=w2_scales[:, cols],
+                rhs=h_codes[:, tok].bitcast(FP8X4),
+                rhs_scale=h_scales[:, tok],
+                start=True,
+                stop=True,
+            )
+            nc.vector.tensor_tensor(gated, bank[:], gate_rows[:, tok], ALU.mult)
 
         def listed(tok):
             return entries(tok.start, tok.stop - tok.start)
 
-        def fetch_block0(tok):
-            nc.scalar.activation(picked[:, tok], window[0][:].indirect(listed(tok)), ACT.Copy)
-
-        def sum_block1(q, gated):
-            summed[q] = keep.tile([P, PIECE], F32, name=f"summed{q}")
-            nc.vector.tensor_tensor(summed[q][:], table1[:].indirect(listed(piece(q))), gated, ALU.add)
-
-        def scatter_on_vector(tok, gated):
-            nc.vector.tensor_tensor(window[0][:].indirect(listed(tok)), picked[:, tok], gated, ALU.add)
+        def sum_on_gpsimd(q):
+            if q == 2:
+                gated = staged.tile([P, PIECE], F32, name="gated12", offset=h_at + 3 * h_bytes)
+            else:
+                gated = keep.tile([P, PIECE], F32, name=f"gated1{q}")
+            second_product(1, piece(q), gated[:])
+            nc.gpsimd.tensor_tensor(summed[:, piece(q)], picked1[:, piece(q - 1)], gated[:], ALU.add)
 
         def store(b, queue):
             for cols in (slice(0, T // 2), slice(T // 2, T)):
@@ -235,34 +226,29 @@ def tile_picked_modres_glusilu_p_kernel(
         )
         quantize_hidden(0)
         hidden(2)
-        fetch_block0(piece(0))
-        fetch_block0(piece(1, PIECES - 1))
+        nc.scalar.activation(picked[:], window[0][:].indirect(offsets[:]), ACT.Copy)
+        picked1 = keep.tile([P, S - PIECE], F32, name="picked1")
+        nc.scalar.activation(picked1[:], window[1][:].indirect(listed(piece(1, PIECES - 1))), ACT.Copy)
         hidden(3)
-        first = keep.tile([P, BLOCKS, PIECE], F32, name="first")
-        second_product((0, 1), piece(0), first)
-        shared_sum = keep.tile([P, PIECE], F32, name="shared_sum")
-        nc.gpsimd.tensor_tensor(shared_sum[:], picked[:, piece(0)], first[:, 0, :], ALU.add)
+        first = staged.tile([P, PIECE], F32, name="first", offset=h_at + 3 * h_bytes + gap // 2)
+        second_product(1, piece(0), first[:])
         quantize_hidden(1)
-        sum_block1(0, first[:, 1, :])
         hidden(4)
-        g1 = gated_block1(1)
+        sum_on_gpsimd(1)
         hidden(5)
-        sum_block1(1, g1[:, 0, :])
+        nc.vector.tensor_tensor(summed[:, piece(0)], window[1][:].indirect(listed(piece(0))), first[:], ALU.add)
         quantize_hidden(2)
         hidden(6)
         hidden(7)
-        g2 = gated_block1(2)
+        sum_on_gpsimd(2)
         quantize_hidden(3)
-        sum_block1(2, g2[:, 0, :])
-        late_pair = staged.tile([P, 1, 2 * PIECE], F32, name="late_pair", offset=h_at + 3 * h_bytes)
-        second_product((0,), piece(1, 2), late_pair)
-        g3 = gated_block1(3)
-        late_last = second_product((0,), piece(3), keep.tile([P, 1, PIECE], F32, name="late_last"))
-        sum_block1(3, g3[:, 0, :])
-        nc.scalar.activation(window[0][:].indirect(listed(piece(0))), shared_sum[:], ACT.Copy)
-        for q in range(PIECES):
-            nc.scalar.activation(window[1][:].indirect(listed(piece(q))), summed[q][:], ACT.Copy)
+        gated0 = staged.tile([P, S], F32, name="gated0", offset=h_offset[3])
+        second_product(0, piece(0, 2), gated0[:, piece(0, 2)])
+        sum_on_gpsimd(3)
+        second_product(0, piece(2, 2), gated0[:, piece(2, 2)])
+        for first_entry, count in ((0, PIECE), (PIECE, LONG), (PIECE + LONG, LONG)):
+            tok = slice(first_entry, first_entry + count)
+            nc.scalar.activation(window[1][:].indirect(listed(tok)), summed[:, tok], ACT.Copy)
         store(1, nc.scalar)
-        scatter_on_vector(piece(3), late_last[:, 0, :])
-        scatter_on_vector(piece(1, 2), late_pair[:, 0, :])
+        nc.vector.tensor_tensor(window[0][:].indirect(offsets[:]), picked[:], gated0[:], ALU.add)
         store(0, nc.sync)

@@ -24,7 +24,8 @@ PIECES = S // PIECE
 BLOCKS = N // P
 RUN = 2
 LONG = 384
-EARLY = 3 * PIECE
+LATE = slice(3 * P, 5 * P)
+W3_AT = 32768
 
 
 def tile_picked_modres_glusilu_p_kernel(
@@ -79,13 +80,14 @@ def tile_picked_modres_glusilu_p_kernel(
             nc.sync.dma_start(window[b][:], res[b * P : (b + 1) * P, :])
 
         x_codes = keep.tile([P, S], U16, name="x_codes", align_bytes=64)
-        x_scale = keep.tile([P, EARLY], U8, name="x_scale", align_bytes=64)
+        x_scale = keep.tile([P, S], U8, name="x_scale", align_bytes=64)
         for half in range(2):
             nc.vector.tensor_copy(
                 x_codes[:, half * (S // 2) : (half + 1) * (S // 2)],
                 word_table[:].indirect(entries(half * (S // 2), S // 2)),
             )
-        nc.vector.tensor_copy(x_scale[:], scale_table[:].indirect(entries(0, EARLY)))
+        for tok in (slice(0, LATE.start), slice(LATE.stop, S)):
+            nc.vector.tensor_copy(x_scale[:, tok], scale_table[:].indirect(entries(tok.start, tok.stop - tok.start)))
 
         def cast(copy, grouped, source, first_run, places):
             runs = source.shape[2] // (PACK * RUN)
@@ -95,7 +97,7 @@ def tile_picked_modres_glusilu_p_kernel(
 
         grouped = {
             "w1": keep.tile([P, PACK * H], BF16, name="w1_grouped", tag="w1_grouped", align_bytes=64),
-            "w3": keep.tile([P, PACK * H], BF16, name="w3_grouped", tag="w3_grouped", align_bytes=64),
+            "w3": staged.tile([P, PACK * H], BF16, name="w3_grouped", offset=W3_AT, align_bytes=64),
         }
         codes = {}
         scales = {}
@@ -117,20 +119,20 @@ def tile_picked_modres_glusilu_p_kernel(
                 ALU.add,
             )
         quantize_first("w1")
-        x_scale_late = keep.tile([P, S - EARLY], U8, name="x_scale_late", tag="w1_grouped", align_bytes=64)
-        nc.vector.tensor_copy(x_scale_late[:], scale_table[:].indirect(entries(EARLY, S - EARLY)))
         cast(nc.scalar.copy, grouped["w3"], w3_raw[0][:], 0, slice(0, 4))
         cast(nc.scalar.copy, grouped["w3"], w3_raw[1][:, :, 0 : H // 2], half_runs, slice(0, 2))
         cast(nc.vector.tensor_copy, grouped["w3"], w3_raw[1][:, :, 0 : H // 2], half_runs, slice(2, 4))
         quantize_first("w3")
+        x_scale_late = staged.tile([P, PIECE], U8, name="x_scale_late", offset=W3_AT + 2048, align_bytes=64)
+        nc.vector.tensor_copy(x_scale_late[:], scale_table[:].indirect(entries(LATE.start, PIECE)))
 
         def first_product(name, c):
             bank = psum.tile([P, PACK, P], F32, name=f"{name}_bank", bufs=4)
             tok = slice(c * P, (c + 1) * P)
-            if tok.start < EARLY:
-                tok_scale = x_scale[:, tok]
+            if LATE.start <= tok.start < LATE.stop:
+                tok_scale = x_scale_late[:, tok.start - LATE.start : tok.stop - LATE.start]
             else:
-                tok_scale = x_scale_late[:, tok.start - EARLY : tok.stop - EARLY]
+                tok_scale = x_scale[:, tok]
             for t in range(PACK):
                 cols = slice(t * P, (t + 1) * P)
                 nc.tensor.matmul_mx(
@@ -147,10 +149,10 @@ def tile_picked_modres_glusilu_p_kernel(
         act_bytes = P * PACK * 4
         h_at = TILES * act_bytes
         h_bytes = PIECE * PACK * 2
-        gap = PIECE * 4
-        h_offset = [h_at, h_at + h_bytes, h_at + 2 * h_bytes, h_at + 3 * h_bytes + gap]
+        first_at = h_at + 7 * h_bytes // 2
+        h_offset = [h_at, h_at + h_bytes, h_at + 2 * h_bytes, first_at + h_bytes // 2]
         h_grouped = {}
-        h_codes = keep.tile([P, S], U32, name="h_codes", align_bytes=64)
+        h_codes = {}
         h_scales = keep.tile([P, S], U8, name="h_scales", align_bytes=64)
         picked = staged.tile([P, S], F32, name="picked", offset=act_bytes // 2)
         summed = keep.tile([P, S], F32, name="summed")
@@ -172,9 +174,19 @@ def tile_picked_modres_glusilu_p_kernel(
             slot = h_grouped[c // 2][:, (c % 2) * P : (c % 2 + 1) * P, :]
             nc.vector.tensor_tensor(slot, first_product("w3", c), act[c][:], ALU.mult)
 
+        def codes_of(tok):
+            half = tok.start // (S // 2)
+            return h_codes[half][:, tok.start - half * (S // 2) : tok.stop - half * (S // 2)].bitcast(FP8X4)
+
         def quantize_hidden(q):
+            if q == 0:
+                h_codes[0] = keep.tile([P, S // 2], U32, name="h_codes0", align_bytes=64)
+            if q == 2:
+                h_codes[1] = staged.tile(
+                    [P, S // 2], U32, name="h_codes1", offset=first_at - h_bytes // 2, align_bytes=64
+                )
             nc.vector.quantize_mx(
-                h_codes[:, piece(q)].bitcast(FP8X4),
+                codes_of(piece(q)),
                 h_scales[:, piece(q)],
                 h_grouped[q][:].rearrange("p n t -> p (n t)"),
             )
@@ -186,7 +198,7 @@ def tile_picked_modres_glusilu_p_kernel(
                 bank[:],
                 lhsT=w2_codes[:, cols].bitcast(FP8X4),
                 lhsT_scale=w2_scales[:, cols],
-                rhs=h_codes[:, tok].bitcast(FP8X4),
+                rhs=codes_of(tok),
                 rhs_scale=h_scales[:, tok],
                 start=True,
                 stop=True,
@@ -197,18 +209,15 @@ def tile_picked_modres_glusilu_p_kernel(
             return entries(tok.start, tok.stop - tok.start)
 
         def sum_on_gpsimd(q):
-            if q == 2:
-                gated = staged.tile([P, PIECE], F32, name="gated12", offset=h_at + 3 * h_bytes)
-            else:
-                gated = keep.tile([P, PIECE], F32, name=f"gated1{q}")
+            gated = keep.tile([P, PIECE], F32, name=f"gated1{q}")
             second_product(1, piece(q), gated[:])
-            nc.gpsimd.tensor_tensor(summed[:, piece(q)], picked1[:, piece(q - 1)], gated[:], ALU.add)
+            nc.gpsimd.tensor_tensor(summed[:, piece(q)], picked1[:, piece(q - 2)], gated[:], ALU.add)
 
         def store(b, queue):
             for cols in (slice(0, T // 2), slice(T // 2, T)):
                 queue.dma_start(out[b * P : (b + 1) * P, cols], window[b][:, cols])
 
-        w2_grouped = keep.tile([P, N, PACK], BF16, name="w2_grouped", tag="w3_grouped", align_bytes=64)
+        w2_grouped = staged.tile([P, N, PACK], BF16, name="w2_grouped", offset=W3_AT, align_bytes=64)
         nc.gpsimd.tensor_scalar(
             w2_grouped[:], w2_raw[:].rearrange("p j c -> p c j"), 1.0, 0.0, ALU.mult, ALU.add
         )
@@ -227,16 +236,16 @@ def tile_picked_modres_glusilu_p_kernel(
         quantize_hidden(0)
         hidden(2)
         nc.scalar.activation(picked[:], window[0][:].indirect(offsets[:]), ACT.Copy)
-        picked1 = keep.tile([P, S - PIECE], F32, name="picked1")
-        nc.scalar.activation(picked1[:], window[1][:].indirect(listed(piece(1, PIECES - 1))), ACT.Copy)
+        picked1 = keep.tile([P, S // 2], F32, name="picked1")
+        nc.scalar.activation(picked1[:], window[1][:].indirect(listed(piece(2, 2))), ACT.Copy)
         hidden(3)
-        first = staged.tile([P, PIECE], F32, name="first", offset=h_at + 3 * h_bytes + gap // 2)
-        second_product(1, piece(0), first[:])
+        first = staged.tile([P, S // 2], F32, name="first", offset=first_at)
+        second_product(1, piece(0), first[:, piece(0)])
         quantize_hidden(1)
         hidden(4)
-        sum_on_gpsimd(1)
+        second_product(1, piece(1), first[:, piece(1)])
         hidden(5)
-        nc.vector.tensor_tensor(summed[:, piece(0)], window[1][:].indirect(listed(piece(0))), first[:], ALU.add)
+        nc.vector.tensor_tensor(summed[:, piece(0, 2)], window[1][:].indirect(listed(piece(0, 2))), first[:], ALU.add)
         quantize_hidden(2)
         hidden(6)
         hidden(7)
@@ -246,7 +255,7 @@ def tile_picked_modres_glusilu_p_kernel(
         second_product(0, piece(0, 2), gated0[:, piece(0, 2)])
         sum_on_gpsimd(3)
         second_product(0, piece(2, 2), gated0[:, piece(2, 2)])
-        for first_entry, count in ((0, PIECE), (PIECE, LONG), (PIECE + LONG, LONG)):
+        for first_entry, count in ((0, LONG), (LONG, LONG), (2 * LONG, PIECE)):
             tok = slice(first_entry, first_entry + count)
             nc.scalar.activation(window[1][:].indirect(listed(tok)), summed[:, tok], ACT.Copy)
         store(1, nc.scalar)

@@ -75,9 +75,10 @@ def tile_picked_modres_glusilu_p_kernel(
             nc.sync.dma_start(w2_raw[e:P:RUN, :, :], w2_rows[e])
         window = [keep.tile([P, T], F32, name=f"window{b}") for b in range(BLOCKS)]
         gate_rows = keep.tile([P, S], F32, name="gate_rows")
-        nc.sync.dma_start(gate_rows[:], gate)
+        nc.sync.dma_start(gate_rows[:, 0 : S // 2], gate[:, 0 : S // 2])
         for b in range(BLOCKS):
             nc.sync.dma_start(window[b][:], res[b * P : (b + 1) * P, :])
+        nc.sync.dma_start(gate_rows[:, S // 2 : S], gate[:, S // 2 : S])
 
         x_codes = keep.tile([P, S], U16, name="x_codes", align_bytes=64)
         x_scale = keep.tile([P, S], U8, name="x_scale", align_bytes=64)
@@ -191,11 +192,13 @@ def tile_picked_modres_glusilu_p_kernel(
                 h_grouped[q][:].rearrange("p n t -> p (n t)"),
             )
 
-        def second_product(b, tok, gated):
-            bank = psum.tile([P, tok.stop - tok.start], F32, name="y_bank", tag="w1_bank", bufs=4)
+        def y_bank(width):
+            return psum.tile([P, width], F32, name="y_bank", tag="w1_bank", bufs=4)
+
+        def multiply_w2(dst, b, tok):
             cols = slice(b * P, (b + 1) * P)
             nc.tensor.matmul_mx(
-                bank[:],
+                dst,
                 lhsT=w2_codes[:, cols].bitcast(FP8X4),
                 lhsT_scale=w2_scales[:, cols],
                 rhs=codes_of(tok),
@@ -203,6 +206,10 @@ def tile_picked_modres_glusilu_p_kernel(
                 start=True,
                 stop=True,
             )
+
+        def second_product(b, tok, gated):
+            bank = y_bank(tok.stop - tok.start)
+            multiply_w2(bank[:], b, tok)
             nc.vector.tensor_tensor(gated, bank[:], gate_rows[:, tok], ALU.mult)
 
         def listed(tok):
@@ -214,8 +221,7 @@ def tile_picked_modres_glusilu_p_kernel(
             nc.gpsimd.tensor_tensor(summed[:, piece(q)], picked1[:, piece(q - 2)], gated[:], ALU.add)
 
         def store(b, queue):
-            for cols in (slice(0, T // 2), slice(T // 2, T)):
-                queue.dma_start(out[b * P : (b + 1) * P, cols], window[b][:, cols])
+            queue.dma_start(out[b * P : (b + 1) * P, :], window[b][:])
 
         w2_grouped = staged.tile([P, N, PACK], BF16, name="w2_grouped", offset=W3_AT, align_bytes=64)
         nc.gpsimd.tensor_scalar(
@@ -250,11 +256,14 @@ def tile_picked_modres_glusilu_p_kernel(
         hidden(6)
         hidden(7)
         sum_on_gpsimd(2)
+        last_bank = y_bank(2 * PIECE)
+        multiply_w2(last_bank[:, 0:PIECE], 0, piece(2))
         quantize_hidden(3)
         gated0 = staged.tile([P, S], F32, name="gated0", offset=h_offset[3])
         second_product(0, piece(0, 2), gated0[:, piece(0, 2)])
         sum_on_gpsimd(3)
-        second_product(0, piece(2, 2), gated0[:, piece(2, 2)])
+        multiply_w2(last_bank[:, PIECE : 2 * PIECE], 0, piece(3))
+        nc.vector.tensor_tensor(gated0[:, piece(2, 2)], last_bank[:], gate_rows[:, piece(2, 2)], ALU.mult)
         for first_entry, count in ((0, LONG), (LONG, LONG), (2 * LONG, PIECE)):
             tok = slice(first_entry, first_entry + count)
             nc.scalar.activation(window[1][:].indirect(listed(tok)), summed[:, tok], ACT.Copy)

@@ -59,8 +59,10 @@ def tile_picked_modres_glusilu_p_kernel(
         warm = keep.tile([P, 1], F32, name="warm")
         nc.scalar.activation(warm[:], warm_in[:], ACT.Silu)
 
-        w1_raw = keep.tile([P, PACK, H], F32, name="w1_raw")
-        nc.sync.dma_start(w1_raw[:], w1.rearrange("(p j) c -> p j c", j=PACK))
+        w1_raw = [keep.tile([P, PACK, H // 2], F32, name=f"w1_raw{half}") for half in range(2)]
+        for half in range(2):
+            cols = slice(half * (H // 2), (half + 1) * (H // 2))
+            nc.sync.dma_start(w1_raw[half][:], w1.rearrange("(p j) c -> p j c", j=PACK)[:, :, cols])
         w3_raw = [
             keep.tile([P, PACK, H // 2], F32, name="w3_raw0"),
             staged.tile([P, PACK, H // 2 + 32], F32, name="w3_raw1", offset=7 * P * 2),
@@ -81,14 +83,13 @@ def tile_picked_modres_glusilu_p_kernel(
         nc.sync.dma_start(gate_rows[:, S // 2 : S], gate[:, S // 2 : S])
 
         x_codes = keep.tile([P, S], U16, name="x_codes", align_bytes=64)
-        x_scale = keep.tile([P, S], U8, name="x_scale", align_bytes=64)
+        x_scale = {0: keep.tile([P, LATE.start], U8, name="x_scale", align_bytes=64)}
         for half in range(2):
             nc.vector.tensor_copy(
                 x_codes[:, half * (S // 2) : (half + 1) * (S // 2)],
                 word_table[:].indirect(entries(half * (S // 2), S // 2)),
             )
-        for tok in (slice(0, LATE.start), slice(LATE.stop, S)):
-            nc.vector.tensor_copy(x_scale[:, tok], scale_table[:].indirect(entries(tok.start, tok.stop - tok.start)))
+        nc.vector.tensor_copy(x_scale[0][:], scale_table[:].indirect(entries(0, LATE.start)))
 
         def cast(copy, grouped, source, first_run, places):
             runs = source.shape[2] // (PACK * RUN)
@@ -103,37 +104,46 @@ def tile_picked_modres_glusilu_p_kernel(
         codes = {}
         scales = {}
 
-        def quantize_first(name):
+        def quantize_first(name, parts):
             codes[name] = keep.tile([P, H], U32, name=f"{name}_codes", align_bytes=64)
             scales[name] = keep.tile([P, H], U8, name=f"{name}_scales", align_bytes=64)
-            nc.vector.quantize_mx(codes[name][:].bitcast(FP8X4), scales[name][:], grouped[name][:])
+            width = H // parts
+            for first_col in range(0, H, width):
+                cols = slice(first_col, first_col + width)
+                nc.vector.quantize_mx(
+                    codes[name][:, cols].bitcast(FP8X4),
+                    scales[name][:, cols],
+                    grouped[name][:, PACK * cols.start : PACK * cols.stop],
+                )
 
         half_runs = H // (2 * PACK * RUN)
-        cast(nc.scalar.copy, grouped["w1"], w1_raw[:], 0, slice(0, 2))
-        for t in range(2, PACK):
+
+        def cast_on_gpsimd(grouped, source, first_run, places):
+            dst = grouped[:].rearrange("p (t v e j) -> p v t e j", t=PACK, e=RUN, j=PACK)
+            src = source.rearrange("p j (v t e) -> p v t e j", t=PACK, e=RUN)
             nc.gpsimd.tensor_scalar(
-                grouped["w1"][:, t * H : (t + 1) * H].rearrange("p (v e j) -> p v e j", e=RUN, j=PACK),
-                w1_raw[:].rearrange("p j (v t e) -> p t v e j", t=PACK, e=RUN)[:, t],
-                1.0,
-                0.0,
-                ALU.mult,
-                ALU.add,
+                dst[:, first_run : first_run + half_runs, places], src[:, :, places], 1.0, 0.0, ALU.mult, ALU.add
             )
-        quantize_first("w1")
-        cast(nc.scalar.copy, grouped["w3"], w3_raw[0][:], 0, slice(0, 4))
-        cast(nc.scalar.copy, grouped["w3"], w3_raw[1][:, :, 0 : H // 2], half_runs, slice(0, 2))
-        cast(nc.vector.tensor_copy, grouped["w3"], w3_raw[1][:, :, 0 : H // 2], half_runs, slice(2, 4))
-        quantize_first("w3")
-        x_scale_late = staged.tile([P, PIECE], U8, name="x_scale_late", offset=W3_AT + 2048, align_bytes=64)
-        nc.vector.tensor_copy(x_scale_late[:], scale_table[:].indirect(entries(LATE.start, PIECE)))
+
+        for half in range(2):
+            cast(nc.scalar.copy, grouped["w1"], w1_raw[half][:], half * half_runs, slice(0, 2))
+            cast_on_gpsimd(grouped["w1"], w1_raw[half][:], half * half_runs, slice(2, 4))
+        quantize_first("w1", 1)
+        x_scale[LATE.stop] = keep.tile([P, S - LATE.stop], U8, name="x_scale_mid", tag="w1_grouped", align_bytes=64)
+        nc.vector.tensor_copy(x_scale[LATE.stop][:], scale_table[:].indirect(entries(LATE.stop, S - LATE.stop)))
+        cast(nc.scalar.copy, grouped["w3"], w3_raw[0][:], 0, slice(1, 4))
+        cast_on_gpsimd(grouped["w3"], w3_raw[0][:], 0, slice(0, 1))
+        cast(nc.scalar.copy, grouped["w3"], w3_raw[1][:, :, 0 : H // 2], half_runs, slice(2, 4))
+        cast_on_gpsimd(grouped["w3"], w3_raw[1][:, :, 0 : H // 2], half_runs, slice(0, 2))
+        quantize_first("w3", 2)
+        x_scale[LATE.start] = staged.tile([P, PIECE], U8, name="x_scale_late", offset=W3_AT + 2048, align_bytes=64)
+        nc.vector.tensor_copy(x_scale[LATE.start][:], scale_table[:].indirect(entries(LATE.start, PIECE)))
 
         def first_product(name, c):
             bank = psum.tile([P, PACK, P], F32, name=f"{name}_bank", bufs=4)
             tok = slice(c * P, (c + 1) * P)
-            if LATE.start <= tok.start < LATE.stop:
-                tok_scale = x_scale_late[:, tok.start - LATE.start : tok.stop - LATE.start]
-            else:
-                tok_scale = x_scale[:, tok]
+            part = max(first for first in x_scale if first <= tok.start)
+            tok_scale = x_scale[part][:, tok.start - part : tok.stop - part]
             for t in range(PACK):
                 cols = slice(t * P, (t + 1) * P)
                 nc.tensor.matmul_mx(
@@ -223,7 +233,7 @@ def tile_picked_modres_glusilu_p_kernel(
         def store(b, queue):
             queue.dma_start(out[b * P : (b + 1) * P, :], window[b][:])
 
-        w2_grouped = staged.tile([P, N, PACK], BF16, name="w2_grouped", offset=W3_AT, align_bytes=64)
+        w2_grouped = staged.tile([P, N, PACK], BF16, name="w2_grouped", offset=W3_AT + 2048 + PIECE, align_bytes=64)
         nc.gpsimd.tensor_scalar(
             w2_grouped[:], w2_raw[:].rearrange("p j c -> p c j"), 1.0, 0.0, ALU.mult, ALU.add
         )

@@ -59,17 +59,18 @@ def tile_picked_modres_glusilu_p_kernel(
         warm = keep.tile([P, 1], F32, name="warm")
         nc.scalar.activation(warm[:], warm_in[:], ACT.Silu)
 
-        w1_raw = [keep.tile([P, PACK, H // 2], F32, name=f"w1_raw{half}") for half in range(2)]
+        def pair(half):
+            return slice(2 * half, 2 * half + 2)
+
+        w1_raw = [keep.tile([P, 2, H], F32, name=f"w1_raw{half}") for half in range(2)]
         for half in range(2):
-            cols = slice(half * (H // 2), (half + 1) * (H // 2))
-            nc.sync.dma_start(w1_raw[half][:], w1.rearrange("(p j) c -> p j c", j=PACK)[:, :, cols])
+            nc.sync.dma_start(w1_raw[half][:], w1.rearrange("(p j) c -> p j c", j=PACK)[:, pair(half), :])
         w3_raw = [
-            keep.tile([P, PACK, H // 2], F32, name="w3_raw0"),
-            staged.tile([P, PACK, H // 2 + 32], F32, name="w3_raw1", offset=7 * P * 2),
+            keep.tile([P, 2, H], F32, name="w3_raw0"),
+            staged.tile([P, 2, H], F32, name="w3_raw1", offset=P * PACK * 2),
         ]
         for half in range(2):
-            cols = slice(half * (H // 2), (half + 1) * (H // 2))
-            nc.sync.dma_start(w3_raw[half][:, :, 0 : H // 2], w3.rearrange("(p j) c -> p j c", j=PACK)[:, :, cols])
+            nc.sync.dma_start(w3_raw[half][:], w3.rearrange("(p j) c -> p j c", j=PACK)[:, pair(half), :])
 
         w2_raw = keep.tile([P, PACK, N], F32, name="w2_raw", align_bytes=64)
         w2_rows = w2.rearrange("(v t e) c -> e v t c", t=PACK, e=RUN)
@@ -91,11 +92,10 @@ def tile_picked_modres_glusilu_p_kernel(
             )
         nc.vector.tensor_copy(x_scale[0][:], scale_table[:].indirect(entries(0, LATE.start)))
 
-        def cast(copy, grouped, source, first_run, places):
-            runs = source.shape[2] // (PACK * RUN)
+        def cast_on_scalar(grouped, source, half, places):
             dst = grouped[:].rearrange("p (t v e j) -> p v t j e", t=PACK, e=RUN, j=PACK)
             src = source.rearrange("p j (v t e) -> p v t j e", t=PACK, e=RUN)
-            copy(dst[:, first_run : first_run + runs, places], src[:, :, places])
+            nc.scalar.copy(dst[:, :, places, pair(half)], src[:, :, places])
 
         grouped = {
             "w1": keep.tile([P, PACK * H], BF16, name="w1_grouped", tag="w1_grouped", align_bytes=64),
@@ -116,25 +116,22 @@ def tile_picked_modres_glusilu_p_kernel(
                     grouped[name][:, PACK * cols.start : PACK * cols.stop],
                 )
 
-        half_runs = H // (2 * PACK * RUN)
-
-        def cast_on_gpsimd(grouped, source, first_run, places):
-            dst = grouped[:].rearrange("p (t v e j) -> p v t e j", t=PACK, e=RUN, j=PACK)
-            src = source.rearrange("p j (v t e) -> p v t e j", t=PACK, e=RUN)
-            nc.gpsimd.tensor_scalar(
-                dst[:, first_run : first_run + half_runs, places], src[:, :, places], 1.0, 0.0, ALU.mult, ALU.add
-            )
+        def cast_on_gpsimd(grouped, source, half, places):
+            dst = grouped[:].rearrange("p (t v e j) -> p t v e j", t=PACK, e=RUN, j=PACK)
+            src = source.rearrange("p j (v t e) -> p t v e j", t=PACK, e=RUN)
+            for t in range(places.start, places.stop):
+                nc.gpsimd.tensor_scalar(dst[:, t, :, :, pair(half)], src[:, t], 1.0, 0.0, ALU.mult, ALU.add)
 
         for half in range(2):
-            cast(nc.scalar.copy, grouped["w1"], w1_raw[half][:], half * half_runs, slice(0, 2))
-            cast_on_gpsimd(grouped["w1"], w1_raw[half][:], half * half_runs, slice(2, 4))
+            cast_on_scalar(grouped["w1"], w1_raw[half][:], half, slice(0, 2))
+            cast_on_gpsimd(grouped["w1"], w1_raw[half][:], half, slice(2, 4))
         quantize_first("w1", 1)
         x_scale[LATE.stop] = keep.tile([P, S - LATE.stop], U8, name="x_scale_mid", tag="w1_grouped", align_bytes=64)
         nc.vector.tensor_copy(x_scale[LATE.stop][:], scale_table[:].indirect(entries(LATE.stop, S - LATE.stop)))
-        cast(nc.scalar.copy, grouped["w3"], w3_raw[0][:], 0, slice(1, 4))
+        cast_on_scalar(grouped["w3"], w3_raw[0][:], 0, slice(1, 4))
         cast_on_gpsimd(grouped["w3"], w3_raw[0][:], 0, slice(0, 1))
-        cast(nc.scalar.copy, grouped["w3"], w3_raw[1][:, :, 0 : H // 2], half_runs, slice(2, 4))
-        cast_on_gpsimd(grouped["w3"], w3_raw[1][:, :, 0 : H // 2], half_runs, slice(0, 2))
+        cast_on_scalar(grouped["w3"], w3_raw[1][:], 1, slice(2, 4))
+        cast_on_gpsimd(grouped["w3"], w3_raw[1][:], 1, slice(0, 2))
         quantize_first("w3", 2)
         x_scale[LATE.start] = staged.tile([P, PIECE], U8, name="x_scale_late", offset=W3_AT + 2048, align_bytes=64)
         nc.vector.tensor_copy(x_scale[LATE.start][:], scale_table[:].indirect(entries(LATE.start, PIECE)))

from contextlib import ExitStack

import concourse.mybir as mybir

K, T, S, H, N = 512, 2048, 1024, 512, 256
FLOPS = 2 * S * (2 * K * H + H * N)

F32 = mybir.dt.float32
BF16 = mybir.dt.bfloat16
I32 = mybir.dt.int32
U32 = mybir.dt.uint32
U16 = mybir.dt.uint16
U8 = mybir.dt.uint8
FP8X4 = mybir.dt.float8_e4m3fn_x4
FP4X4 = mybir.dt.float4_e2m1fn_x4
ACT = mybir.ActivationFunctionType
ALU = mybir.AluOpType

P = 128
PACK = 4
TILES = S // P
PIECE = 2 * P
PIECES = S // PIECE
BLOCKS = N // P
RUN = 2
LONG = 384
LATE = slice(3 * P, 5 * P)
W3_AT = 32768


def tile_picked_modres_glusilu_p_kernel(
    tc, x_words, x_scales, gate, res, w1, w3, w2, offs, out
):
    nc = tc.nc
    with ExitStack() as ctx:
        keep = ctx.enter_context(tc.tile_pool(name="keep", bufs=1))
        staged = ctx.enter_context(tc.tile_pool(name="staged", bufs=1))
        psum = ctx.enter_context(tc.psum_pool(name="psum", bufs=2))

        offsets = keep.tile([P, S // 16], U16, name="offsets")
        nc.sync.dma_start(offsets[:], offs)

        def entries(first, count):
            return offsets[:, first // 16 : (first + count) // 16]

        word_table = keep.tile([P, T], U16, name="word_table")
        nc.sync.dma_start(word_table[:].bitcast(I32), x_words[0].bitcast(I32))

        scale_table = keep.tile([P, T], U8, name="scale_table")
        nc.gpsimd.memset(scale_table[:].bitcast(I32), 0)
        for q in range(4):
            nc.sync.dma_start(
                scale_table[32 * q : 32 * q + 4, :].bitcast(I32),
                x_scales[0, 4 * q : 4 * q + 4, :].bitcast(I32),
            )

        warm_in = keep.tile([P, 1], F32, name="warm_in")
        nc.gpsimd.memset(warm_in[:], 0.0)
        warm = keep.tile([P, 1], F32, name="warm")
        nc.scalar.activation(warm[:], warm_in[:], ACT.Silu)

        def pair(half):
            return slice(2 * half, 2 * half + 2)

        w1_raw = [keep.tile([P, 2, H], F32, name=f"w1_raw{half}") for half in range(2)]
        for half in range(2):
            nc.sync.dma_start(w1_raw[half][:], w1.rearrange("(p j) c -> p j c", j=PACK)[:, pair(half), :])
        w3_raw = [
            keep.tile([P, 2, H], F32, name="w3_raw0"),
            staged.tile([P, 2, H], F32, name="w3_raw1", offset=P * PACK * 2),
        ]
        for half in range(2):
            nc.sync.dma_start(w3_raw[half][:], w3.rearrange("(p j) c -> p j c", j=PACK)[:, pair(half), :])

        w2_raw = keep.tile([P, PACK, N], F32, name="w2_raw", align_bytes=64)
        w2_rows = w2.rearrange("(v t e) c -> e v t c", t=PACK, e=RUN)
        for e in range(RUN):
            nc.sync.dma_start(w2_raw[e:P:RUN, :, :], w2_rows[e])
        window = [keep.tile([P, T], F32, name=f"window{b}") for b in range(BLOCKS)]
        gate_rows = keep.tile([P, S], F32, name="gate_rows")
        nc.sync.dma_start(gate_rows[:, 0 : S // 2], gate[:, 0 : S // 2])
        for b in range(BLOCKS):
            nc.sync.dma_start(window[b][:], res[b * P : (b + 1) * P, :])
        nc.sync.dma_start(gate_rows[:, S // 2 : S], gate[:, S // 2 : S])

        x_codes = keep.tile([P, S], U16, name="x_codes", align_bytes=64)
        x_scale = {0: keep.tile([P, LATE.start], U8, name="x_scale", align_bytes=64)}
        for half in range(2):
            nc.vector.tensor_copy(
                x_codes[:, half * (S // 2) : (half + 1) * (S // 2)],
                word_table[:].indirect(entries(half * (S // 2), S // 2)),
            )
        nc.vector.tensor_copy(x_scale[0][:], scale_table[:].indirect(entries(0, LATE.start)))

        def cast_on_scalar(grouped, source, half, places):
            dst = grouped[:].rearrange("p (t v e j) -> p v t j e", t=PACK, e=RUN, j=PACK)
            src = source.rearrange("p j (v t e) -> p v t j e", t=PACK, e=RUN)
            nc.scalar.copy(dst[:, :, places, pair(half)], src[:, :, places])

        grouped = {
            "w1": keep.tile([P, PACK * H], BF16, name="w1_grouped", tag="w1_grouped", align_bytes=64),
            "w3": staged.tile([P, PACK * H], BF16, name="w3_grouped", offset=W3_AT, align_bytes=64),
        }
        codes = {}
        scales = {}

        def quantize_first(name, parts):
            codes[name] = keep.tile([P, H], U32, name=f"{name}_codes", align_bytes=64)
            scales[name] = keep.tile([P, H], U8, name=f"{name}_scales", align_bytes=64)
            width = H // parts
            for first_col in range(0, H, width):
                cols = slice(first_col, first_col + width)
                nc.vector.quantize_mx(
                    codes[name][:, cols].bitcast(FP8X4),
                    scales[name][:, cols],
                    grouped[name][:, PACK * cols.start : PACK * cols.stop],
                )

        def cast_on_gpsimd(grouped, source, half, places):
            dst = grouped[:].rearrange("p (t v e j) -> p t v e j", t=PACK, e=RUN, j=PACK)
            src = source.rearrange("p j (v t e) -> p t v e j", t=PACK, e=RUN)
            for t in range(places.start, places.stop):
                nc.gpsimd.tensor_scalar(dst[:, t, :, :, pair(half)], src[:, t], 1.0, 0.0, ALU.mult, ALU.add)

        for half in range(2):
            cast_on_scalar(grouped["w1"], w1_raw[half][:], half, slice(0, 2))
            cast_on_gpsimd(grouped["w1"], w1_raw[half][:], half, slice(2, 4))
        quantize_first("w1", 1)
        x_scale[LATE.stop] = keep.tile([P, S - LATE.stop], U8, name="x_scale_mid", tag="w1_grouped", align_bytes=64)
        nc.vector.tensor_copy(x_scale[LATE.stop][:], scale_table[:].indirect(entries(LATE.stop, S - LATE.stop)))
        cast_on_scalar(grouped["w3"], w3_raw[0][:], 0, slice(1, 4))
        cast_on_gpsimd(grouped["w3"], w3_raw[0][:], 0, slice(0, 1))
        cast_on_scalar(grouped["w3"], w3_raw[1][:], 1, slice(2, 4))
        cast_on_gpsimd(grouped["w3"], w3_raw[1][:], 1, slice(0, 2))
        quantize_first("w3", 2)
        x_scale[LATE.start] = staged.tile([P, PIECE], U8, name="x_scale_late", offset=W3_AT + 2048, align_bytes=64)
        nc.vector.tensor_copy(x_scale[LATE.start][:], scale_table[:].indirect(entries(LATE.start, PIECE)))

        def first_product(name, c):
            bank = psum.tile([P, PACK, P], F32, name=f"{name}_bank", bufs=4)
            tok = slice(c * P, (c + 1) * P)
            part = max(first for first in x_scale if first <= tok.start)
            tok_scale = x_scale[part][:, tok.start - part : tok.stop - part]
            for t in range(PACK):
                cols = slice(t * P, (t + 1) * P)
                nc.tensor.matmul_mx(
                    bank[:, t, :],
                    lhsT=codes[name][:, cols].bitcast(FP8X4),
                    lhsT_scale=scales[name][:, cols],
                    rhs=x_codes[:, tok].bitcast(FP4X4),
                    rhs_scale=tok_scale,
                    start=True,
                    stop=True,
                )
            return bank[:].rearrange("p t n -> p n t")

        act_bytes = P * PACK * 4
        h_at = TILES * act_bytes
        h_bytes = PIECE * PACK * 2
        first_at = h_at + 7 * h_bytes // 2
        h_offset = [h_at, h_at + h_bytes, h_at + 2 * h_bytes, first_at + h_bytes // 2]
        h_grouped = {}
        h_codes = {}
        h_scales = keep.tile([P, S], U8, name="h_scales", align_bytes=64)
        picked = staged.tile([P, S], F32, name="picked", offset=act_bytes // 2)
        summed = keep.tile([P, S], F32, name="summed")

        def piece(q, count=1):
            return slice(q * PIECE, (q + count) * PIECE)

        act = {}

        def silu(c):
            act[c] = staged.tile([P, P, PACK], F32, name=f"act{c}", offset=c * act_bytes)
            nc.scalar.activation(act[c][:], first_product("w1", c), ACT.Silu)

        def hidden(c):
            if c % 2 == 0:
                h_grouped[c // 2] = staged.tile(
                    [P, PIECE, PACK], BF16, name=f"h_grouped{c // 2}", offset=h_offset[c // 2], align_bytes=64
                )
            slot = h_grouped[c // 2][:, (c % 2) * P : (c % 2 + 1) * P, :]
            nc.vector.tensor_tensor(slot, first_product("w3", c), act[c][:], ALU.mult)

        def codes_of(tok):
            half = tok.start // (S // 2)
            return h_codes[half][:, tok.start - half * (S // 2) : tok.stop - half * (S // 2)].bitcast(FP8X4)

        def quantize_hidden(q):
            if q == 0:
                h_codes[0] = keep.tile([P, S // 2], U32, name="h_codes0", align_bytes=64)
            if q == 2:
                h_codes[1] = staged.tile(
                    [P, S // 2], U32, name="h_codes1", offset=first_at - h_bytes // 2, align_bytes=64
                )
            nc.vector.quantize_mx(
                codes_of(piece(q)),
                h_scales[:, piece(q)],
                h_grouped[q][:].rearrange("p n t -> p (n t)"),
            )

        def y_bank(width):
            return psum.tile([P, width], F32, name="y_bank", tag="w1_bank", bufs=4)

        def multiply_w2(dst, b, tok):
            cols = slice(b * P, (b + 1) * P)
            nc.tensor.matmul_mx(
                dst,
                lhsT=w2_codes[:, cols].bitcast(FP8X4),
                lhsT_scale=w2_scales[:, cols],
                rhs=codes_of(tok),
                rhs_scale=h_scales[:, tok],
                start=True,
                stop=True,
            )

        def second_product(b, tok, gated):
            bank = y_bank(tok.stop - tok.start)
            multiply_w2(bank[:], b, tok)
            nc.vector.tensor_tensor(gated, bank[:], gate_rows[:, tok], ALU.mult)

        def listed(tok):
            return entries(tok.start, tok.stop - tok.start)

        def sum_on_gpsimd(q):
            gated = keep.tile([P, PIECE], F32, name=f"gated1{q}")
            second_product(1, piece(q), gated[:])
            nc.gpsimd.tensor_tensor(summed[:, piece(q)], picked1[:, piece(q - 2)], gated[:], ALU.add)

        def store(b, queue):
            queue.dma_start(out[b * P : (b + 1) * P, :], window[b][:])

        w2_grouped = staged.tile([P, N, PACK], BF16, name="w2_grouped", offset=W3_AT + 2048 + PIECE, align_bytes=64)
        nc.gpsimd.tensor_scalar(
            w2_grouped[:], w2_raw[:].rearrange("p j c -> p c j"), 1.0, 0.0, ALU.mult, ALU.add
        )
        w2_codes = keep.tile([P, N], U32, name="w2_codes", align_bytes=64)
        w2_scales = keep.tile([P, N], U8, name="w2_scales", align_bytes=64)

        for c in range(4):
            silu(c)
        hidden(0)
        hidden(1)
        for c in range(4, TILES):
            silu(c)
        nc.vector.quantize_mx(
            w2_codes[:].bitcast(FP8X4), w2_scales[:], w2_grouped[:].rearrange("p c j -> p (c j)")
        )
        quantize_hidden(0)
        hidden(2)
        nc.scalar.activation(picked[:], window[0][:].indirect(offsets[:]), ACT.Copy)
        picked1 = keep.tile([P, S // 2], F32, name="picked1")
        nc.scalar.activation(picked1[:], window[1][:].indirect(listed(piece(2, 2))), ACT.Copy)
        hidden(3)
        first = staged.tile([P, S // 2], F32, name="first", offset=first_at)
        second_product(1, piece(0), first[:, piece(0)])
        quantize_hidden(1)
        hidden(4)
        second_product(1, piece(1), first[:, piece(1)])
        hidden(5)
        nc.vector.tensor_tensor(summed[:, piece(0, 2)], window[1][:].indirect(listed(piece(0, 2))), first[:], ALU.add)
        quantize_hidden(2)
        hidden(6)
        hidden(7)
        sum_on_gpsimd(2)
        last_bank = y_bank(2 * PIECE)
        multiply_w2(last_bank[:, 0:PIECE], 0, piece(2))
        quantize_hidden(3)
        gated0 = staged.tile([P, S], F32, name="gated0", offset=h_offset[3])
        second_product(0, piece(0, 2), gated0[:, piece(0, 2)])
        sum_on_gpsimd(3)
        multiply_w2(last_bank[:, PIECE : 2 * PIECE], 0, piece(3))
        nc.vector.tensor_tensor(gated0[:, piece(2, 2)], last_bank[:], gate_rows[:, piece(2, 2)], ALU.mult)
        for first_entry, count in ((0, LONG), (LONG, LONG), (2 * LONG, PIECE)):
            tok = slice(first_entry, first_entry + count)
            nc.scalar.activation(window[1][:].indirect(listed(tok)), summed[:, tok], ACT.Copy)
        store(1, nc.scalar)
        nc.vector.tensor_tensor(window[0][:].indirect(offsets[:]), picked[:], gated0[:], ALU.add)
        store(0, nc.sync)
